import numpy as np
import ml_dtypes


def mxq(x, axis, fmt="e4m3"):
    dtype, down = {"e4m3": (ml_dtypes.float8_e4m3fn, 7), "e5m2": (ml_dtypes.float8_e5m2, 14)}[fmt]
    v = np.moveaxis(np.asarray(x, np.float32).astype(ml_dtypes.bfloat16).astype(np.float64), axis, -1)
    blocks = v.reshape(v.shape[:-1] + (-1, 32))
    amax = np.abs(blocks).max(-1, keepdims=True)
    byte = np.maximum(np.where(amax > 0, np.frexp(amax)[1] - 1 + 127, 0) - down, 1)
    scale = np.exp2(byte - 127.0)
    codes = (blocks / scale).astype(np.float32).astype(dtype).astype(np.float64)
    return np.moveaxis((codes * scale).reshape(v.shape), -1, axis)


WIDE = False


def mx_kscale(k):
    if not WIDE:
        return np.ones(k)
    levels = np.array([10, -10, 5, -5, 0])
    if k % 512:
        return np.exp2(np.random.permutation(np.resize(levels, k // 32))).repeat(32)
    a = np.empty((k // 512, 16))
    for p in range(k // 512):
        a[p, :8] = np.random.permutation(np.resize(levels, 8))
        for g in range(8):
            far = levels[np.abs(levels - a[p, g]) >= 10]
            a[p, g + 8] = far[np.random.randint(len(far))]
    return np.exp2(a.ravel()).repeat(32)


def f64(x):
    return np.asarray(x).astype(np.float64)


def striped(idx):
    return np.tile(idx.reshape(-1, 16).T, (8, 1)).astype(np.uint16)


def unstriped(offs):
    return offs[:16].T.reshape(-1).astype(np.int64)


E2M1 = np.array([0.0, 0.5, 1.0, 1.5, 2.0, 3.0, 4.0, 6.0, -0.0, -0.5, -1.0, -1.5, -2.0, -3.0, -4.0, -6.0])


def pack_weight(w, fmt):
    k, n = w.shape
    w = f64(np.asarray(w, np.float32).astype(ml_dtypes.bfloat16)).reshape(k // 32, 32, n)
    amax = np.abs(w).max(1)
    if fmt == "e4m3":
        byte = np.frexp(amax)[1] - 1 + 127 - 7
    else:
        mant, ex = np.frexp(amax / 6.0)
        byte = np.where(mant > 0.5, ex, ex - 1) + 127
    byte = np.clip(np.where(amax > 0, byte, 1), 1, 254)
    scaled = (w * np.exp2(127.0 - byte)[:, None, :]).reshape(k, n).astype(np.float32)
    by_word = np.ascontiguousarray(scaled.reshape(k // 512, 128, 4, n).transpose(0, 1, 3, 2))
    if fmt == "e4m3":
        words = by_word.astype(ml_dtypes.float8_e4m3fn).view(np.uint8)
    else:
        c = by_word.astype(ml_dtypes.float4_e2m1fn).view(np.uint8) & 0xF
        words = (c[..., 0::2] | (c[..., 1::2] << 4)).reshape(k // 512, 128, 2 * n)
    return np.ascontiguousarray(words), np.ascontiguousarray(byte.astype(np.uint8).reshape(k // 512, 16, n))


def unpack_weight(words, scales, fmt):
    g, _, n = scales.shape
    words = np.ascontiguousarray(words).reshape(g, 128, n, -1)
    if fmt == "e4m3":
        vals = words.view(ml_dtypes.float8_e4m3fn).astype(np.float64)
    else:
        nib = np.empty((g, 128, n, 4), np.uint8)
        nib[..., 0::2] = words & 0xF
        nib[..., 1::2] = words >> 4
        vals = E2M1[nib]
    vals = vals * np.repeat(np.exp2(scales.astype(np.float64) - 127.0), 8, axis=1)[..., None]
    return vals.transpose(0, 1, 3, 2).reshape(g * 512, n)


def silu(v):
    return v / (1.0 + np.exp(-np.maximum(v, -700.0)))


K, T, E, C, H, N = 512, 640, 5, 256, 512, 128


def by_expert(wq, xq):
    return np.concatenate([wq[e].T @ xq[:, e * C:(e + 1) * C] for e in range(E)], axis=1)


def setup_inputs():
    n = np.random.standard_normal
    s = mx_kscale(K)
    u = mx_kscale(H)
    first = np.random.permutation(np.repeat(np.arange(E), T // E))
    second = (first + 1 + np.random.permutation(np.repeat(np.arange(E - 1), -(-T // (E - 1)))[:T])) % E
    while np.bincount(second, minlength=E).max() != T // E:
        load = np.bincount(second, minlength=E); hi, lo = int(load.argmax()), int(load.argmin())
        t = np.flatnonzero((second == hi) & (first != lo))[0]; second[t] = lo
    slot_token = np.empty(E * C, np.int64); pos = np.empty((2, T), np.int64); fill = np.zeros(E, np.int64)
    place = np.stack([np.random.permutation(C) for _ in range(E)])
    for r, deal in enumerate((first, second)):
        for t in np.random.permutation(T):
            e = deal[t]; j = e * C + place[e, fill[e]]; fill[e] += 1; slot_token[j] = t; pos[r, t] = j
    g = np.random.uniform(0.2, 0.8, T)
    x = pack_weight(n((K, T)) * s[:, None], "e4m3")
    wg = pack_weight(n((K, N)) / np.sqrt(K) / s[:, None], "e2m1")
    return {
        "x_words": x[0],
        "x_scales": x[1],
        "wg_words": wg[0],
        "wg_scales": wg[1],
        "w1": (n((E, K, H)) / np.sqrt(K) / s[None, :, None] * u).astype(np.float32),
        "w2": (n((E, H, N)) / np.sqrt(H) / u[None, :, None]).astype(np.float32),
        "gate": np.stack([np.tile(g, (128, 1)), np.tile(1.0 - g, (128, 1))]).astype(np.float32),
        "offs": striped(slot_token),
        "pos1": striped(pos[0]),
        "pos2": striped(pos[1]),
    }


def reference(x_words, x_scales, wg_words, wg_scales, w1, w2, gate, offs, pos1, pos2):
    wg = unpack_weight(wg_words, wg_scales, "e2m1")
    w1q = mxq(f64(w1), 1, "e4m3")
    w2q = mxq(f64(w2), 1, "e4m3")
    idx = unstriped(offs)
    x = unpack_weight(x_words, x_scales, "e4m3")
    o = silu(wg.T @ x)
    h = silu(by_expert(w1q, x[:, idx]))
    y = by_expert(w2q, mxq(h, 0, "e4m3"))
    c = sum(f64(gate[r, :1]) * y[:, unstriped(p)] for r, p in enumerate((pos1, pos2)))
    return o * c

@@ -1,0 +1,262 @@
+from contextlib import ExitStack
+
+import concourse.mybir as mybir
+
+K, T, E, C, H, N = 512, 640, 5, 256, 512, 128
+S = E * C
+FLOPS = 2 * K * N * T + 2 * S * (K * H + H * N)
+
+F32 = mybir.dt.float32
+BF16 = mybir.dt.bfloat16
+I32 = mybir.dt.int32
+U32 = mybir.dt.uint32
+U16 = mybir.dt.uint16
+U8 = mybir.dt.uint8
+FP8X4 = mybir.dt.float8_e4m3fn_x4
+FP4X4 = mybir.dt.float4_e2m1fn_x4
+SILU = mybir.ActivationFunctionType.Silu
+MULT = mybir.AluOpType.mult
+ADD = mybir.AluOpType.add
+
+P = 128
+PACK = 4
+HALF = 128
+W1_CUTS = [[["S",0,64],["S",64,96],["S",96,128]],[["V",0,120],["S",120,128]],[["S",0,24],["S",24,80],["V",80,128]],[["S",0,32],["V",32,96],["S",96,128]],[["S",0,40],["V",40,88],["V",88,128]]]
+W2_CAST = "VSVVV"
+Y_COPY = "SSSSS"
+GATE_PRODUCT = "VV"
+SECOND_PIECES = [1,1,1,1,1]
+TAIL = [[0,512],[512,640]]
+GATHER_CUTS = [[0,384],[384,832],[832,1280]]
+SHARED = {}
+
+
+def tile_moe_ogt_silu_silu_kernel(
+    tc, x_words, x_scales, wg_words, wg_scales, w1, w2, gate, offs, pos1, pos2, out
+):
+    nc = tc.nc
+    with ExitStack() as ctx:
+        keep = ctx.enter_context(tc.tile_pool(name="keep", bufs=1))
+        psum_h = ctx.enter_context(tc.psum_pool(name="psum_h", bufs=4))
+        psum_y = ctx.enter_context(tc.psum_pool(name="psum_y", bufs=2))
+        psum_o = ctx.enter_context(tc.psum_pool(name="psum_o", bufs=1))
+        tiles = {}
+
+        def sb(name, shape, dtype):
+            tiles[name] = keep.tile(shape, dtype, name=name, tag=SHARED.get(name, name), align_bytes=64)
+            return tiles[name]
+
+        def copy_on(engine, dst, src):
+            if engine == "S":
+                nc.scalar.copy(out=dst, in_=src)
+            elif engine == "V":
+                nc.vector.tensor_copy(out=dst, in_=src)
+            else:
+                nc.gpsimd.tensor_copy(out=dst, in_=src)
+
+        offs_t = sb("offs_t", [P, S // 16], U16)
+        pos_t = [sb("pos1_t", [P, T // 16], U16), sb("pos2_t", [P, T // 16], U16)]
+        xw = sb("xw", [P, T], U32)
+        xs = sb("xs", [P, T], U8)
+        wgw = sb("wgw", [P, 2 * N], U8)
+        wgs = sb("wgs", [P, N], U8)
+        w1_raw = [sb("w1r%d" % e, [P, PACK, H], F32) for e in range(E)]
+        w2_raw = [sb("w2r%d" % e, [P, PACK, N], F32) for e in range(E)]
+        gate_t = sb("gate_t", [P, 2, T], F32)
+        y = sb("y", [P, S], F32)
+        picked = sb("picked", [P, 2, T], F32)
+        res = sb("res", [P, T], F32)
+
+        def load_w1(e, lo, hi):
+            nc.sync.dma_start(
+                out=w1_raw[e][:, :, lo:hi], in_=w1[e].rearrange("(p j) c -> p j c", j=PACK)[:, :, lo:hi]
+            )
+
+        def load_w2(e):
+            nc.sync.dma_start(out=w2_raw[e][:], in_=w2[e].rearrange("(p j) c -> p j c", j=PACK))
+
+        def load_scales(eng, plane, rows):
+            for q in range(4):
+                four = rows[0, 4 * q : 4 * q + 4, :].bitcast(I32)
+                eng.dma_start(
+                    out=plane[32 * q : 32 * q + 32, :].bitcast(I32),
+                    in_=four.unsqueeze(0).to_broadcast([8, 4, four.shape[1]]),
+                )
+
+        nc.scalar.dma_start(out=wgw[:].bitcast(I32), in_=wg_words[0].bitcast(I32))
+        load_scales(nc.scalar, wgs, wg_scales)
+        nc.sync.dma_start(offs_t[:], offs)
+        nc.sync.dma_start(out=xw[:].bitcast(I32), in_=x_words[0].rearrange("p t d -> p (t d)").bitcast(I32))
+        load_w1(0, 0, 256)
+        load_scales(nc.sync, xs, x_scales)
+        load_w1(0, 256, 512)
+        load_w1(2, 0, 512)
+        load_w1(1, 0, 512)
+        load_w1(3, 0, 512)
+        load_w1(4, 0, 512)
+        load_w2(4)
+        load_w2(0)
+        load_w2(2)
+        load_w2(1)
+        load_w2(3)
+        nc.sync.dma_start(pos_t[0][:], pos1)
+        nc.sync.dma_start(pos_t[1][:], pos2)
+        nc.sync.dma_start(out=gate_t[:], in_=gate.rearrange("r p t -> p r t"))
+
+        warm = sb("warm", [P, 8], F32)
+        nc.vector.memset(warm[:, 0:1], 0.0)
+        nc.scalar.activation(warm[:, 4:5], warm[:, 0:1], SILU)
+
+        xg = sb("xg", [P, S], U32)
+        xgs = sb("xgs", [P, S], U8)
+
+        def gather_words(i):
+            lo, hi = GATHER_CUTS[i]
+            nc.vector.tensor_copy(xg[:, lo:hi], xw[:].indirect(offs_t[:, lo // 16 : hi // 16]))
+
+        def gather_scales(i):
+            lo, hi = GATHER_CUTS[i]
+            nc.vector.tensor_copy(xgs[:, lo:hi], xs[:].indirect(offs_t[:, lo // 16 : hi // 16]))
+
+        def cast_w1(e):
+            src = w1_raw[e][:].rearrange("p j (m t) -> p m j t", t=PACK)
+            dst = sb("w1b%d" % e, [P, PACK, P, PACK], BF16)[:].rearrange("p t m j -> p m j t")
+            for engine, lo, hi in W1_CUTS[e]:
+                copy_on(engine, dst[:, lo:hi], src[:, lo:hi])
+
+        def quant_w1(e):
+            nc.vector.quantize_mx(
+                out=sb("w1c%d" % e, [P, H], U32)[:].bitcast(FP8X4),
+                scales=sb("w1s%d" % e, [P, H], U8)[:],
+                in_=tiles["w1b%d" % e][:].rearrange("p t m j -> p (t m j)"),
+            )
+
+        def cast_w2(e):
+            src = w2_raw[e][:].rearrange("p j (c i) -> p c j i", i=4)
+            dst = sb("w2b%d" % e, [P, N, PACK], BF16)[:].rearrange("p (c i) j -> p c j i", i=4)
+            copy_on(W2_CAST[e], dst, src)
+
+        def quant_w2(e):
+            nc.vector.quantize_mx(
+                out=sb("w2c%d" % e, [P, N], U32)[:].bitcast(FP8X4),
+                scales=sb("w2s%d" % e, [P, N], U8)[:],
+                in_=tiles["w2b%d" % e][:].rearrange("p n j -> p (n j)"),
+            )
+
+        def first_layer(e):
+            h_b = sb("hb%d" % e, [P, C, PACK], BF16)
+            for u in range(C // HALF):
+                cols = slice(u * HALF, (u + 1) * HALF)
+                slots = slice(e * C + u * HALF, e * C + (u + 1) * HALF)
+                bank = psum_h.tile([P, PACK, HALF], F32, name="h_bank")
+                for t in range(PACK):
+                    ch = slice(t * P, (t + 1) * P)
+                    nc.tensor.matmul_mx(
+                        out=bank[:, t, :],
+                        lhsT=tiles["w1c%d" % e][:, ch].bitcast(FP8X4),
+                        lhsT_scale=tiles["w1s%d" % e][:, ch],
+                        rhs=xg[:, slots].bitcast(FP8X4),
+                        rhs_scale=xgs[:, slots],
+                        start=True,
+                        stop=True,
+                    )
+                nc.scalar.activation(h_b[:, cols, :], bank[:].rearrange("p t n -> p n t"), SILU)
+
+        def second_layer(e):
+            h_c = sb("hc%d" % e, [P, C], U32)
+            h_s = sb("hs%d" % e, [P, C], U8)
+            width = C // SECOND_PIECES[e]
+            for lo in range(0, C, width):
+                cols = slice(lo, lo + width)
+                nc.vector.quantize_mx(
+                    out=h_c[:, cols].bitcast(FP8X4),
+                    scales=h_s[:, cols],
+                    in_=tiles["hb%d" % e][:, cols, :].rearrange("p n t -> p (n t)"),
+                )
+                bank = psum_y.tile([P, width], F32, name="y_bank")
+                nc.tensor.matmul_mx(
+                    out=bank[:],
+                    lhsT=tiles["w2c%d" % e][:].bitcast(FP8X4),
+                    lhsT_scale=tiles["w2s%d" % e][:],
+                    rhs=h_c[:, cols].bitcast(FP8X4),
+                    rhs_scale=h_s[:, cols],
+                    start=True,
+                    stop=True,
+                )
+                copy_on(Y_COPY[e], y[:, e * C + lo : e * C + lo + width], bank[:])
+
+        def output_gate():
+            o = sb("o0", [P, T], F32)
+            for name, lo, hi in (("o_bank0", 0, 512), ("o_bank1", 512, T)):
+                bank = psum_o.tile([P, hi - lo], F32, name=name)
+                nc.tensor.matmul_mx(
+                    out=bank[:],
+                    lhsT=wgw[:].bitcast(FP4X4),
+                    lhsT_scale=wgs[:],
+                    rhs=xw[:, lo:hi].bitcast(FP8X4),
+                    rhs_scale=xs[:, lo:hi],
+                    start=True,
+                    stop=True,
+                )
+                nc.scalar.activation(o[:, lo:hi], bank[:], SILU)
+
+        def gate_products():
+            og = sb("og0", [P, 2, T], F32)
+            for r in range(2):
+                engine = nc.vector if GATE_PRODUCT[r] == "V" else nc.gpsimd
+                engine.tensor_tensor(og[:, r, :], tiles["o0"][:], gate_t[:, r, :], MULT)
+
+        cast_w2(3)
+        cast_w1(0)
+        quant_w1(0)
+        gather_words(2)
+        gather_words(1)
+        quant_w2(3)
+        output_gate()
+        cast_w1(2)
+        cast_w1(1)
+        gather_words(0)
+        gather_scales(0)
+        cast_w1(4)
+        cast_w2(0)
+        gather_scales(1)
+        quant_w2(0)
+        first_layer(0)
+        gate_products()
+        second_layer(0)
+        quant_w1(1)
+        cast_w2(1)
+        quant_w1(2)
+        gather_scales(2)
+        quant_w1(4)
+        first_layer(2)
+        quant_w2(1)
+        cast_w1(3)
+        first_layer(1)
+        cast_w2(2)
+        quant_w2(2)
+        second_layer(1)
+        first_layer(4)
+        quant_w1(3)
+        second_layer(2)
+        cast_w2(4)
+        quant_w2(4)
+        second_layer(4)
+        first_layer(3)
+        second_layer(3)
+
+        def pick(r, lo, hi):
+            nc.vector.tensor_tensor(
+                picked[:, r, lo:hi], y[:].indirect(pos_t[r][:, lo // 16 : hi // 16]), tiles["og0"][:, r, lo:hi], MULT
+            )
+
+        def finish(lo, hi):
+            nc.vector.tensor_tensor(res[:, lo:hi], picked[:, 0, lo:hi], picked[:, 1, lo:hi], ADD)
+            nc.sync.dma_start(out=out[:, lo:hi], in_=res[:, lo:hi])
+
+        for i, (lo, hi) in enumerate(TAIL):
+            pick(0, lo, hi)
+            if i > 0:
+                finish(*TAIL[i - 1])
+            pick(1, lo, hi)
+        finish(*TAIL[-1])

@@ -21,13 +21,14 @@ ADD = mybir.AluOpType.add
 P = 128
 PACK = 4
 HALF = 128
-W1_CUTS = [[["S",0,64],["S",64,96],["S",96,128]],[["V",0,120],["S",120,128]],[["S",0,24],["S",24,80],["V",80,128]],[["S",0,32],["V",32,96],["S",96,128]],[["S",0,40],["V",40,88],["V",88,128]]]
-W2_CAST = "VSVVV"
+W1_CUTS = [[["S",0,8],["S",8,72],["S",72,128]],[["S",0,128]],[["V",0,64],["V",64,104],["V",104,128]],[["V",0,32],["V",32,112],["S",112,128]],[["S",0,48],["V",48,128]]]
+W2_CAST = "VVVSS"
 Y_COPY = "SSSSS"
 GATE_PRODUCT = "VV"
-SECOND_PIECES = [1,1,1,1,1]
+SECOND_PIECES = [2,2,2,1,1]
 TAIL = [[0,512],[512,640]]
-GATHER_CUTS = [[0,384],[384,832],[832,1280]]
+GATHER_CUTS = [[0,384],[384,800],[800,1280]]
+W2_GROUPS = [[0,2],[2,4],[4,5]]
 SHARED = {}
 
 
@@ -41,6 +42,7 @@ def tile_moe_ogt_silu_silu_kernel(
         psum_y = ctx.enter_context(tc.psum_pool(name="psum_y", bufs=2))
         psum_o = ctx.enter_context(tc.psum_pool(name="psum_o", bufs=1))
         tiles = {}
+        w2_mx = {}
 
         def sb(name, shape, dtype):
             tiles[name] = keep.tile(shape, dtype, name=name, tag=SHARED.get(name, name), align_bytes=64)
@@ -61,7 +63,7 @@ def tile_moe_ogt_silu_silu_kernel(
         wgw = sb("wgw", [P, 2 * N], U8)
         wgs = sb("wgs", [P, N], U8)
         w1_raw = [sb("w1r%d" % e, [P, PACK, H], F32) for e in range(E)]
-        w2_raw = [sb("w2r%d" % e, [P, PACK, N], F32) for e in range(E)]
+        w2_raw = [sb("w2r%d" % g, [P, hi - lo, PACK, N], F32) for g, (lo, hi) in enumerate(W2_GROUPS)]
         gate_t = sb("gate_t", [P, 2, T], F32)
         y = sb("y", [P, S], F32)
         picked = sb("picked", [P, 2, T], F32)
@@ -72,8 +74,9 @@ def tile_moe_ogt_silu_silu_kernel(
                 out=w1_raw[e][:, :, lo:hi], in_=w1[e].rearrange("(p j) c -> p j c", j=PACK)[:, :, lo:hi]
             )
 
-        def load_w2(e):
-            nc.sync.dma_start(out=w2_raw[e][:], in_=w2[e].rearrange("(p j) c -> p j c", j=PACK))
+        def load_w2(g):
+            lo, hi = W2_GROUPS[g]
+            nc.sync.dma_start(out=w2_raw[g][:], in_=w2[lo:hi].rearrange("e (p j) c -> p e j c", j=PACK))
 
         def load_scales(eng, plane, rows):
             for q in range(4):
@@ -83,22 +86,19 @@ def tile_moe_ogt_silu_silu_kernel(
                     in_=four.unsqueeze(0).to_broadcast([8, 4, four.shape[1]]),
                 )
 
-        nc.scalar.dma_start(out=wgw[:].bitcast(I32), in_=wg_words[0].bitcast(I32))
-        load_scales(nc.scalar, wgs, wg_scales)
-        nc.sync.dma_start(offs_t[:], offs)
+        load_scales(nc.scalar, xs, x_scales)
         nc.sync.dma_start(out=xw[:].bitcast(I32), in_=x_words[0].rearrange("p t d -> p (t d)").bitcast(I32))
-        load_w1(0, 0, 256)
-        load_scales(nc.sync, xs, x_scales)
-        load_w1(0, 256, 512)
-        load_w1(2, 0, 512)
+        nc.sync.dma_start(offs_t[:], offs)
+        load_w1(0, 0, 512)
         load_w1(1, 0, 512)
+        load_w1(2, 0, 512)
+        load_w2(0)
         load_w1(3, 0, 512)
         load_w1(4, 0, 512)
-        load_w2(4)
-        load_w2(0)
-        load_w2(2)
         load_w2(1)
-        load_w2(3)
+        nc.scalar.dma_start(out=wgw[:].bitcast(I32), in_=wg_words[0].bitcast(I32))
+        load_scales(nc.scalar, wgs, wg_scales)
+        load_w2(2)
         nc.sync.dma_start(pos_t[0][:], pos1)
         nc.sync.dma_start(pos_t[1][:], pos2)
         nc.sync.dma_start(out=gate_t[:], in_=gate.rearrange("r p t -> p r t"))
@@ -131,17 +131,22 @@ def tile_moe_ogt_silu_silu_kernel(
                 in_=tiles["w1b%d" % e][:].rearrange("p t m j -> p (t m j)"),
             )
 
-        def cast_w2(e):
-            src = w2_raw[e][:].rearrange("p j (c i) -> p c j i", i=4)
-            dst = sb("w2b%d" % e, [P, N, PACK], BF16)[:].rearrange("p (c i) j -> p c j i", i=4)
-            copy_on(W2_CAST[e], dst, src)
+        def cast_w2(g):
+            lo, hi = W2_GROUPS[g]
+            src = w2_raw[g][:].rearrange("p e j (c i) -> p e c j i", i=4)
+            dst = sb("w2b%d" % g, [P, hi - lo, N, PACK], BF16)[:].rearrange("p e (c i) j -> p e c j i", i=4)
+            copy_on(W2_CAST[g], dst, src)
 
-        def quant_w2(e):
+        def quant_w2(g):
+            lo, hi = W2_GROUPS[g]
+            codes = sb("w2c%d" % g, [P, (hi - lo) * N], U32)
+            scales = sb("w2s%d" % g, [P, (hi - lo) * N], U8)
             nc.vector.quantize_mx(
-                out=sb("w2c%d" % e, [P, N], U32)[:].bitcast(FP8X4),
-                scales=sb("w2s%d" % e, [P, N], U8)[:],
-                in_=tiles["w2b%d" % e][:].rearrange("p n j -> p (n j)"),
+                out=codes[:].bitcast(FP8X4), scales=scales[:], in_=tiles["w2b%d" % g][:].rearrange("p e n j -> p (e n j)")
             )
+            for e in range(lo, hi):
+                cols = slice((e - lo) * N, (e - lo + 1) * N)
+                w2_mx[e] = (codes[:, cols], scales[:, cols])
 
         def first_layer(e):
             h_b = sb("hb%d" % e, [P, C, PACK], BF16)
@@ -176,8 +181,8 @@ def tile_moe_ogt_silu_silu_kernel(
                 bank = psum_y.tile([P, width], F32, name="y_bank")
                 nc.tensor.matmul_mx(
                     out=bank[:],
-                    lhsT=tiles["w2c%d" % e][:].bitcast(FP8X4),
-                    lhsT_scale=tiles["w2s%d" % e][:],
+                    lhsT=w2_mx[e][0].bitcast(FP8X4),
+                    lhsT_scale=w2_mx[e][1],
                     rhs=h_c[:, cols].bitcast(FP8X4),
                     rhs_scale=h_s[:, cols],
                     start=True,
@@ -206,44 +211,40 @@ def tile_moe_ogt_silu_silu_kernel(
                 engine = nc.vector if GATE_PRODUCT[r] == "V" else nc.gpsimd
                 engine.tensor_tensor(og[:, r, :], tiles["o0"][:], gate_t[:, r, :], MULT)
 
-        cast_w2(3)
         cast_w1(0)
         quant_w1(0)
-        gather_words(2)
-        gather_words(1)
-        quant_w2(3)
-        output_gate()
-        cast_w1(2)
-        cast_w1(1)
         gather_words(0)
         gather_scales(0)
-        cast_w1(4)
-        cast_w2(0)
         gather_scales(1)
-        quant_w2(0)
-        first_layer(0)
-        gate_products()
-        second_layer(0)
+        cast_w1(1)
+        gather_words(1)
+        cast_w1(2)
         quant_w1(1)
-        cast_w2(1)
+        cast_w2(0)
         quant_w1(2)
-        gather_scales(2)
-        quant_w1(4)
-        first_layer(2)
-        quant_w2(1)
-        cast_w1(3)
+        output_gate()
+        first_layer(0)
         first_layer(1)
-        cast_w2(2)
-        quant_w2(2)
-        second_layer(1)
-        first_layer(4)
+        cast_w1(3)
+        quant_w2(0)
+        second_layer(0)
         quant_w1(3)
-        second_layer(2)
-        cast_w2(4)
-        quant_w2(4)
-        second_layer(4)
+        gather_scales(2)
+        cast_w1(4)
+        first_layer(2)
+        second_layer(1)
+        quant_w1(4)
+        gather_words(2)
+        cast_w2(1)
+        cast_w2(2)
         first_layer(3)
+        quant_w2(1)
+        first_layer(4)
+        second_layer(2)
+        quant_w2(2)
         second_layer(3)
+        second_layer(4)
+        gate_products()
 
         def pick(r, lo, hi):
             nc.vector.tensor_tensor(

@@ -20,16 +20,16 @@ ADD = mybir.AluOpType.add
 
 P = 128
 PACK = 4
-HALF = 128
-W1_CUTS = [[["S",0,8],["S",8,72],["S",72,128]],[["S",0,128]],[["V",0,64],["V",64,104],["V",104,128]],[["V",0,32],["V",32,112],["S",112,128]],[["S",0,48],["V",48,128]]]
-W2_CAST = "VVVSS"
-Y_COPY = "SSSSS"
-GATE_PRODUCT = "VV"
-SECOND_PIECES = [2,2,2,1,1]
-TAIL = [[0,512],[512,640]]
-GATHER_CUTS = [[0,384],[384,800],[800,1280]]
-W2_GROUPS = [[0,2],[2,4],[4,5]]
-SHARED = {}
+LIST_ROWS = 16
+BANK = 512
+BANK_SLOTS = BANK // PACK
+FIRST_BANKS = 4
+SECOND_BANKS = 2
+
+W1_ON_VECTOR = ((0, 16), (0, 0), (0, 128), (16, 128), (48, 128))
+GATHER_CUTS = ((0, 448), (448, 896), (896, S))
+GROUPS = ((0, 2), (2, 4), (4, 5))
+TOKEN_CUTS = ((0, 512), (512, T))
 
 
 def tile_moe_ogt_silu_silu_kernel(
@@ -38,226 +38,154 @@ def tile_moe_ogt_silu_silu_kernel(
     nc = tc.nc
     with ExitStack() as ctx:
         keep = ctx.enter_context(tc.tile_pool(name="keep", bufs=1))
-        psum_h = ctx.enter_context(tc.psum_pool(name="psum_h", bufs=4))
-        psum_y = ctx.enter_context(tc.psum_pool(name="psum_y", bufs=2))
-        psum_o = ctx.enter_context(tc.psum_pool(name="psum_o", bufs=1))
-        tiles = {}
-        w2_mx = {}
+        psum = ctx.enter_context(tc.psum_pool(name="psum", bufs=1))
 
-        def sb(name, shape, dtype):
-            tiles[name] = keep.tile(shape, dtype, name=name, tag=SHARED.get(name, name), align_bytes=64)
-            return tiles[name]
+        def sbuf(name, shape, dtype):
+            return keep.tile(shape, dtype, name=name, align_bytes=64)
 
-        def copy_on(engine, dst, src):
-            if engine == "S":
-                nc.scalar.copy(out=dst, in_=src)
-            elif engine == "V":
-                nc.vector.tensor_copy(out=dst, in_=src)
-            else:
-                nc.gpsimd.tensor_copy(out=dst, in_=src)
-
-        offs_t = sb("offs_t", [P, S // 16], U16)
-        pos_t = [sb("pos1_t", [P, T // 16], U16), sb("pos2_t", [P, T // 16], U16)]
-        xw = sb("xw", [P, T], U32)
-        xs = sb("xs", [P, T], U8)
-        wgw = sb("wgw", [P, 2 * N], U8)
-        wgs = sb("wgs", [P, N], U8)
-        w1_raw = [sb("w1r%d" % e, [P, PACK, H], F32) for e in range(E)]
-        w2_raw = [sb("w2r%d" % g, [P, hi - lo, PACK, N], F32) for g, (lo, hi) in enumerate(W2_GROUPS)]
-        gate_t = sb("gate_t", [P, 2, T], F32)
-        y = sb("y", [P, S], F32)
-        picked = sb("picked", [P, 2, T], F32)
-        res = sb("res", [P, T], F32)
-
-        def load_w1(e, lo, hi):
-            nc.sync.dma_start(
-                out=w1_raw[e][:, :, lo:hi], in_=w1[e].rearrange("(p j) c -> p j c", j=PACK)[:, :, lo:hi]
+        def mx_matmul(dst, stationary, moving):
+            nc.tensor.matmul_mx(
+                out=dst,
+                lhsT=stationary[0],
+                lhsT_scale=stationary[1],
+                rhs=moving[0],
+                rhs_scale=moving[1],
+                start=True,
+                stop=True,
             )
 
-        def load_w2(g):
-            lo, hi = W2_GROUPS[g]
-            nc.sync.dma_start(out=w2_raw[g][:], in_=w2[lo:hi].rearrange("e (p j) c -> p e j c", j=PACK))
+        def quantize(words, scales, values):
+            nc.vector.quantize_mx(out=words.bitcast(FP8X4), scales=scales, in_=values)
 
-        def load_scales(eng, plane, rows):
+        first_banks = [psum.tile([P, BANK], F32, name="first_bank%d" % b) for b in range(FIRST_BANKS)]
+        second_banks = [psum.tile([P, BANK], F32, name="second_bank%d" % b) for b in range(SECOND_BANKS)]
+
+        offs_t = sbuf("offs_t", [P, S // LIST_ROWS], U16)
+        pos_t = [sbuf("pos1_t", [P, T // LIST_ROWS], U16), sbuf("pos2_t", [P, T // LIST_ROWS], U16)]
+        x_w = sbuf("x_w", [P, T], U32)
+        x_s = sbuf("x_s", [P, T], U8)
+        wg_w = sbuf("wg_w", [P, 2 * N], U8)
+        wg_s = sbuf("wg_s", [P, N], U8)
+        w1_raw = [sbuf("w1_raw%d" % e, [P, PACK, H], F32) for e in range(E)]
+        w2_raw = sbuf("w2_raw", [P, E, PACK, N], F32)
+        gate_t = sbuf("gate_t", [P, 2, T], F32)
+        slot_w = sbuf("slot_w", [P, S], U32)
+        slot_s = sbuf("slot_s", [P, S], U8)
+        w1_b = [sbuf("w1_b%d" % e, [P, PACK, P, PACK], BF16) for e in range(E)]
+        w1_w = [sbuf("w1_w%d" % e, [P, H], U32) for e in range(E)]
+        w1_s = [sbuf("w1_s%d" % e, [P, H], U8) for e in range(E)]
+        w2_b = sbuf("w2_b", [P, E, N, PACK], BF16)
+        w2_w = sbuf("w2_w", [P, E * N], U32)
+        w2_s = sbuf("w2_s", [P, E * N], U8)
+        h_b = sbuf("h_b", [P, S, PACK], BF16)
+        h_w = sbuf("h_w", [P, S], U32)
+        h_s = sbuf("h_s", [P, S], U8)
+        y = sbuf("y", [P, S], F32)
+        o = sbuf("o", [P, T], F32)
+        gated = sbuf("gated", [P, 2, T], F32)
+        picked = sbuf("picked", [P, 2, T], F32)
+        res = sbuf("res", [P, T], F32)
+
+        warm = sbuf("warm", [P, 2], F32)
+        nc.vector.memset(warm[:, 0:1], 0.0)
+        nc.scalar.activation(warm[:, 1:2], warm[:, 0:1], SILU)
+
+        def load_scale_rows(dst, rows):
             for q in range(4):
                 four = rows[0, 4 * q : 4 * q + 4, :].bitcast(I32)
-                eng.dma_start(
-                    out=plane[32 * q : 32 * q + 32, :].bitcast(I32),
+                nc.scalar.dma_start(
+                    out=dst[32 * q : 32 * q + 32, :].bitcast(I32),
                     in_=four.unsqueeze(0).to_broadcast([8, 4, four.shape[1]]),
                 )
 
-        load_scales(nc.scalar, xs, x_scales)
-        nc.sync.dma_start(out=xw[:].bitcast(I32), in_=x_words[0].rearrange("p t d -> p (t d)").bitcast(I32))
+        nc.sync.dma_start(out=x_w[:].bitcast(I32), in_=x_words[0].rearrange("p t d -> p (t d)").bitcast(I32))
         nc.sync.dma_start(offs_t[:], offs)
-        load_w1(0, 0, 512)
-        load_w1(1, 0, 512)
-        load_w1(2, 0, 512)
-        load_w2(0)
-        load_w1(3, 0, 512)
-        load_w1(4, 0, 512)
-        load_w2(1)
-        nc.scalar.dma_start(out=wgw[:].bitcast(I32), in_=wg_words[0].bitcast(I32))
-        load_scales(nc.scalar, wgs, wg_scales)
-        load_w2(2)
+        load_scale_rows(x_s, x_scales)
+        nc.scalar.dma_start(out=wg_w[:].bitcast(I32), in_=wg_words[0].bitcast(I32))
+        load_scale_rows(wg_s, wg_scales)
+        for e in range(E):
+            nc.sync.dma_start(out=w1_raw[e][:], in_=w1[e].rearrange("(p j) c -> p j c", j=PACK))
+        for lo, hi in GROUPS:
+            nc.sync.dma_start(out=w2_raw[:, lo:hi], in_=w2[lo:hi].rearrange("e (p j) c -> p e j c", j=PACK))
         nc.sync.dma_start(pos_t[0][:], pos1)
         nc.sync.dma_start(pos_t[1][:], pos2)
         nc.sync.dma_start(out=gate_t[:], in_=gate.rearrange("r p t -> p r t"))
 
-        warm = sb("warm", [P, 8], F32)
-        nc.vector.memset(warm[:, 0:1], 0.0)
-        nc.scalar.activation(warm[:, 4:5], warm[:, 0:1], SILU)
+        for lo, hi in GATHER_CUTS:
+            entries = offs_t[:, lo // LIST_ROWS : hi // LIST_ROWS]
+            nc.vector.tensor_copy(slot_w[:, lo:hi], x_w[:].indirect(entries))
+            nc.vector.tensor_copy(slot_s[:, lo:hi], x_s[:].indirect(entries))
 
-        xg = sb("xg", [P, S], U32)
-        xgs = sb("xgs", [P, S], U8)
-
-        def gather_words(i):
-            lo, hi = GATHER_CUTS[i]
-            nc.vector.tensor_copy(xg[:, lo:hi], xw[:].indirect(offs_t[:, lo // 16 : hi // 16]))
-
-        def gather_scales(i):
-            lo, hi = GATHER_CUTS[i]
-            nc.vector.tensor_copy(xgs[:, lo:hi], xs[:].indirect(offs_t[:, lo // 16 : hi // 16]))
-
-        def cast_w1(e):
+        def round_w1(e):
             src = w1_raw[e][:].rearrange("p j (m t) -> p m j t", t=PACK)
-            dst = sb("w1b%d" % e, [P, PACK, P, PACK], BF16)[:].rearrange("p t m j -> p m j t")
-            for engine, lo, hi in W1_CUTS[e]:
-                copy_on(engine, dst[:, lo:hi], src[:, lo:hi])
+            dst = w1_b[e][:].rearrange("p t m j -> p m j t")
+            lo, hi = W1_ON_VECTOR[e]
+            if lo > 0:
+                nc.scalar.copy(out=dst[:, 0:lo], in_=src[:, 0:lo])
+            if hi > lo:
+                nc.vector.tensor_copy(out=dst[:, lo:hi], in_=src[:, lo:hi])
+            if hi < P:
+                nc.scalar.copy(out=dst[:, hi:P], in_=src[:, hi:P])
 
-        def quant_w1(e):
-            nc.vector.quantize_mx(
-                out=sb("w1c%d" % e, [P, H], U32)[:].bitcast(FP8X4),
-                scales=sb("w1s%d" % e, [P, H], U8)[:],
-                in_=tiles["w1b%d" % e][:].rearrange("p t m j -> p (t m j)"),
+        round_w1(0)
+        for e in range(E):
+            if e + 1 < E:
+                round_w1(e + 1)
+            quantize(w1_w[e][:], w1_s[e][:], w1_b[e][:].rearrange("p t m j -> p (t m j)"))
+
+        gate_pieces = ((0, BANK), (BANK, T))
+        for turn, (lo, hi) in enumerate(gate_pieces):
+            bank = first_banks[turn][:, 0 : hi - lo]
+            mx_matmul(bank, (wg_w[:].bitcast(FP4X4), wg_s[:]), (x_w[:, lo:hi].bitcast(FP8X4), x_s[:, lo:hi]))
+            nc.scalar.activation(o[:, lo:hi], bank, SILU)
+
+        for lo, hi in GROUPS:
+            nc.vector.tensor_copy(
+                out=w2_b[:, lo:hi].rearrange("p e (c d) j -> p e c j d", d=4),
+                in_=w2_raw[:, lo:hi].rearrange("p e j (c d) -> p e c j d", d=4),
             )
 
-        def cast_w2(g):
-            lo, hi = W2_GROUPS[g]
-            src = w2_raw[g][:].rearrange("p e j (c i) -> p e c j i", i=4)
-            dst = sb("w2b%d" % g, [P, hi - lo, N, PACK], BF16)[:].rearrange("p e (c i) j -> p e c j i", i=4)
-            copy_on(W2_CAST[g], dst, src)
+        for piece in range(S // BANK_SLOTS):
+            slots = slice(piece * BANK_SLOTS, (piece + 1) * BANK_SLOTS)
+            e = slots.start // C
+            bank = first_banks[(len(gate_pieces) + piece) % FIRST_BANKS][:].rearrange("p (t s) -> p t s", t=PACK)
+            for t in range(PACK):
+                cols = slice(t * P, (t + 1) * P)
+                mx_matmul(
+                    bank[:, t, :],
+                    (w1_w[e][:, cols].bitcast(FP8X4), w1_s[e][:, cols]),
+                    (slot_w[:, slots].bitcast(FP8X4), slot_s[:, slots]),
+                )
+            nc.scalar.activation(h_b[:, slots, :], bank.rearrange("p t s -> p s t"), SILU)
 
-        def quant_w2(g):
-            lo, hi = W2_GROUPS[g]
-            codes = sb("w2c%d" % g, [P, (hi - lo) * N], U32)
-            scales = sb("w2s%d" % g, [P, (hi - lo) * N], U8)
-            nc.vector.quantize_mx(
-                out=codes[:].bitcast(FP8X4), scales=scales[:], in_=tiles["w2b%d" % g][:].rearrange("p e n j -> p (e n j)")
-            )
+        for turn, (lo, hi) in enumerate(GROUPS):
+            group_cols, group_slots = slice(lo * N, hi * N), slice(lo * C, hi * C)
+            quantize(w2_w[:, group_cols], w2_s[:, group_cols], w2_b[:, lo:hi].rearrange("p e n j -> p (e n j)"))
+            quantize(h_w[:, group_slots], h_s[:, group_slots], h_b[:, group_slots, :].rearrange("p s t -> p (s t)"))
+            bank = second_banks[turn % SECOND_BANKS]
             for e in range(lo, hi):
-                cols = slice((e - lo) * N, (e - lo + 1) * N)
-                w2_mx[e] = (codes[:, cols], scales[:, cols])
-
-        def first_layer(e):
-            h_b = sb("hb%d" % e, [P, C, PACK], BF16)
-            for u in range(C // HALF):
-                cols = slice(u * HALF, (u + 1) * HALF)
-                slots = slice(e * C + u * HALF, e * C + (u + 1) * HALF)
-                bank = psum_h.tile([P, PACK, HALF], F32, name="h_bank")
-                for t in range(PACK):
-                    ch = slice(t * P, (t + 1) * P)
-                    nc.tensor.matmul_mx(
-                        out=bank[:, t, :],
-                        lhsT=tiles["w1c%d" % e][:, ch].bitcast(FP8X4),
-                        lhsT_scale=tiles["w1s%d" % e][:, ch],
-                        rhs=xg[:, slots].bitcast(FP8X4),
-                        rhs_scale=xgs[:, slots],
-                        start=True,
-                        stop=True,
-                    )
-                nc.scalar.activation(h_b[:, cols, :], bank[:].rearrange("p t n -> p n t"), SILU)
-
-        def second_layer(e):
-            h_c = sb("hc%d" % e, [P, C], U32)
-            h_s = sb("hs%d" % e, [P, C], U8)
-            width = C // SECOND_PIECES[e]
-            for lo in range(0, C, width):
-                cols = slice(lo, lo + width)
-                nc.vector.quantize_mx(
-                    out=h_c[:, cols].bitcast(FP8X4),
-                    scales=h_s[:, cols],
-                    in_=tiles["hb%d" % e][:, cols, :].rearrange("p n t -> p (n t)"),
+                cols, slots = slice(e * N, (e + 1) * N), slice(e * C, (e + 1) * C)
+                mx_matmul(
+                    bank[:, (e - lo) * C : (e - lo + 1) * C],
+                    (w2_w[:, cols].bitcast(FP8X4), w2_s[:, cols]),
+                    (h_w[:, slots].bitcast(FP8X4), h_s[:, slots]),
                 )
-                bank = psum_y.tile([P, width], F32, name="y_bank")
-                nc.tensor.matmul_mx(
-                    out=bank[:],
-                    lhsT=w2_mx[e][0].bitcast(FP8X4),
-                    lhsT_scale=w2_mx[e][1],
-                    rhs=h_c[:, cols].bitcast(FP8X4),
-                    rhs_scale=h_s[:, cols],
-                    start=True,
-                    stop=True,
-                )
-                copy_on(Y_COPY[e], y[:, e * C + lo : e * C + lo + width], bank[:])
+            nc.scalar.copy(out=y[:, group_slots], in_=bank[:, 0 : (hi - lo) * C])
 
-        def output_gate():
-            o = sb("o0", [P, T], F32)
-            for name, lo, hi in (("o_bank0", 0, 512), ("o_bank1", 512, T)):
-                bank = psum_o.tile([P, hi - lo], F32, name=name)
-                nc.tensor.matmul_mx(
-                    out=bank[:],
-                    lhsT=wgw[:].bitcast(FP4X4),
-                    lhsT_scale=wgs[:],
-                    rhs=xw[:, lo:hi].bitcast(FP8X4),
-                    rhs_scale=xs[:, lo:hi],
-                    start=True,
-                    stop=True,
-                )
-                nc.scalar.activation(o[:, lo:hi], bank[:], SILU)
-
-        def gate_products():
-            og = sb("og0", [P, 2, T], F32)
-            for r in range(2):
-                engine = nc.vector if GATE_PRODUCT[r] == "V" else nc.gpsimd
-                engine.tensor_tensor(og[:, r, :], tiles["o0"][:], gate_t[:, r, :], MULT)
-
-        cast_w1(0)
-        quant_w1(0)
-        gather_words(0)
-        gather_scales(0)
-        gather_scales(1)
-        cast_w1(1)
-        gather_words(1)
-        cast_w1(2)
-        quant_w1(1)
-        cast_w2(0)
-        quant_w1(2)
-        output_gate()
-        first_layer(0)
-        first_layer(1)
-        cast_w1(3)
-        quant_w2(0)
-        second_layer(0)
-        quant_w1(3)
-        gather_scales(2)
-        cast_w1(4)
-        first_layer(2)
-        second_layer(1)
-        quant_w1(4)
-        gather_words(2)
-        cast_w2(1)
-        cast_w2(2)
-        first_layer(3)
-        quant_w2(1)
-        first_layer(4)
-        second_layer(2)
-        quant_w2(2)
-        second_layer(3)
-        second_layer(4)
-        gate_products()
+        for r in range(2):
+            nc.vector.tensor_tensor(gated[:, r, :], o[:], gate_t[:, r, :], MULT)
 
         def pick(r, lo, hi):
-            nc.vector.tensor_tensor(
-                picked[:, r, lo:hi], y[:].indirect(pos_t[r][:, lo // 16 : hi // 16]), tiles["og0"][:, r, lo:hi], MULT
-            )
+            entries = pos_t[r][:, lo // LIST_ROWS : hi // LIST_ROWS]
+            nc.vector.tensor_tensor(picked[:, r, lo:hi], y[:].indirect(entries), gated[:, r, lo:hi], MULT)
 
-        def finish(lo, hi):
+        def add_and_store(lo, hi):
             nc.vector.tensor_tensor(res[:, lo:hi], picked[:, 0, lo:hi], picked[:, 1, lo:hi], ADD)
             nc.sync.dma_start(out=out[:, lo:hi], in_=res[:, lo:hi])
 
-        for i, (lo, hi) in enumerate(TAIL):
+        for i, (lo, hi) in enumerate(TOKEN_CUTS):
             pick(0, lo, hi)
             if i > 0:
-                finish(*TAIL[i - 1])
+                add_and_store(*TOKEN_CUTS[i - 1])
             pick(1, lo, hi)
-        finish(*TAIL[-1])
+        add_and_store(*TOKEN_CUTS[-1])

@@ -1,3 +1,4 @@
+import functools
 from contextlib import ExitStack
 
 import concourse.mybir as mybir
@@ -26,10 +27,10 @@ BANK_SLOTS = BANK // PACK
 FIRST_BANKS = 4
 SECOND_BANKS = 2
 
-W1_ON_VECTOR = ((0, 16), (0, 0), (0, 128), (16, 128), (48, 128))
-GATHER_CUTS = ((0, 448), (448, 896), (896, S))
+W1_ON_VECTOR = ((0, 0), (0, 64), (P, 64), (P, 40), (P, 40))
+WINDOW = 1408
 GROUPS = ((0, 2), (2, 4), (4, 5))
-TOKEN_CUTS = ((0, 512), (512, T))
+TOKEN_CUTS = ((0, T // 2), (T // 2, T))
 
 
 def tile_moe_ogt_silu_silu_kernel(
@@ -40,8 +41,8 @@ def tile_moe_ogt_silu_silu_kernel(
         keep = ctx.enter_context(tc.tile_pool(name="keep", bufs=1))
         psum = ctx.enter_context(tc.psum_pool(name="psum", bufs=1))
 
-        def sbuf(name, shape, dtype):
-            return keep.tile(shape, dtype, name=name, align_bytes=64)
+        def sbuf(name, shape, dtype, tag=None):
+            return keep.tile(shape, dtype, name=name, tag=tag or name, align_bytes=64)
 
         def mx_matmul(dst, stationary, moving):
             nc.tensor.matmul_mx(
@@ -59,133 +60,174 @@ def tile_moe_ogt_silu_silu_kernel(
 
         first_banks = [psum.tile([P, BANK], F32, name="first_bank%d" % b) for b in range(FIRST_BANKS)]
         second_banks = [psum.tile([P, BANK], F32, name="second_bank%d" % b) for b in range(SECOND_BANKS)]
+        gate_banks = [psum.tile([P, BANK], F32, name="gate_bank%d" % b) for b in range(2)]
 
         offs_t = sbuf("offs_t", [P, S // LIST_ROWS], U16)
         pos_t = [sbuf("pos1_t", [P, T // LIST_ROWS], U16), sbuf("pos2_t", [P, T // LIST_ROWS], U16)]
-        x_w = sbuf("x_w", [P, T], U32)
-        x_s = sbuf("x_s", [P, T], U8)
+        x_w = sbuf("x_w", [P, WINDOW], U32)
+        x_s = sbuf("x_s", [P, WINDOW], U8)
         wg_w = sbuf("wg_w", [P, 2 * N], U8)
         wg_s = sbuf("wg_s", [P, N], U8)
         w1_raw = [sbuf("w1_raw%d" % e, [P, PACK, H], F32) for e in range(E)]
-        w2_raw = sbuf("w2_raw", [P, E, PACK, N], F32)
+        w2_raw = [sbuf("w2_raw%d" % lo, [P, hi - lo, PACK, N], F32) for lo, hi in GROUPS]
         gate_t = sbuf("gate_t", [P, 2, T], F32)
-        slot_w = sbuf("slot_w", [P, S], U32)
-        slot_s = sbuf("slot_s", [P, S], U8)
-        w1_b = [sbuf("w1_b%d" % e, [P, PACK, P, PACK], BF16) for e in range(E)]
+        slot_w = sbuf("slot_w", [P, S - C], U32)
+        slot_s = sbuf("slot_s", [P, S - C], U8)
+        w1_b = [[sbuf("w1_b%d_%d" % (e, u), [P, 2, P, PACK], BF16) for u in range(2)] for e in range(E)]
         w1_w = [sbuf("w1_w%d" % e, [P, H], U32) for e in range(E)]
         w1_s = [sbuf("w1_s%d" % e, [P, H], U8) for e in range(E)]
-        w2_b = sbuf("w2_b", [P, E, N, PACK], BF16)
+        w2_b = [sbuf("w2_b%d" % lo, [P, hi - lo, N, PACK], BF16) for lo, hi in GROUPS]
         w2_w = sbuf("w2_w", [P, E * N], U32)
         w2_s = sbuf("w2_s", [P, E * N], U8)
-        h_b = sbuf("h_b", [P, S, PACK], BF16)
-        h_w = sbuf("h_w", [P, S], U32)
         h_s = sbuf("h_s", [P, S], U8)
         y = sbuf("y", [P, S], F32)
         o = sbuf("o", [P, T], F32)
-        gated = sbuf("gated", [P, 2, T], F32)
         picked = sbuf("picked", [P, 2, T], F32)
+        both = sbuf("both", [P, T], F32)
         res = sbuf("res", [P, T], F32)
+
+        def load_scale_rows(queues, dst, rows):
+            for q, queue in enumerate(queues):
+                four = rows[0, 4 * q : 4 * q + 4, :].bitcast(I32)
+                queue.dma_start(
+                    out=dst[32 * q : 32 * q + 32, :].bitcast(I32),
+                    in_=four.unsqueeze(0).to_broadcast([8, 4, four.shape[1]]),
+                )
+
+        nc.sync.dma_start(out=x_w[:, 0:T].bitcast(I32), in_=x_words[0].rearrange("p t d -> p (t d)").bitcast(I32))
+        nc.sync.dma_start(offs_t[:], offs)
+        load_scale_rows((nc.scalar, nc.scalar, nc.sync, nc.sync), x_s[:, 0:T], x_scales)
+        for e in range(E):
+            nc.sync.dma_start(out=w1_raw[e][:], in_=w1[e].rearrange("(p j) c -> p j c", j=PACK))
+        for g, (lo, hi) in enumerate(GROUPS):
+            nc.sync.dma_start(out=w2_raw[g][:], in_=w2[lo:hi].rearrange("e (p j) c -> p e j c", j=PACK))
+        nc.sync.dma_start(out=wg_w[:].bitcast(I32), in_=wg_words[0].bitcast(I32))
+        load_scale_rows((nc.sync,) * 4, wg_s[:], wg_scales)
+        nc.sync.dma_start(pos_t[0][:], pos1)
+        nc.sync.dma_start(pos_t[1][:], pos2)
+        nc.sync.dma_start(out=gate_t[:], in_=gate.rearrange("r p t -> p r t"))
 
         warm = sbuf("warm", [P, 2], F32)
         nc.vector.memset(warm[:, 0:1], 0.0)
         nc.scalar.activation(warm[:, 1:2], warm[:, 0:1], SILU)
 
-        def load_scale_rows(dst, rows):
-            for q in range(4):
-                four = rows[0, 4 * q : 4 * q + 4, :].bitcast(I32)
-                nc.scalar.dma_start(
-                    out=dst[32 * q : 32 * q + 32, :].bitcast(I32),
-                    in_=four.unsqueeze(0).to_broadcast([8, 4, four.shape[1]]),
-                )
-
-        nc.sync.dma_start(out=x_w[:].bitcast(I32), in_=x_words[0].rearrange("p t d -> p (t d)").bitcast(I32))
-        nc.sync.dma_start(offs_t[:], offs)
-        load_scale_rows(x_s, x_scales)
-        nc.scalar.dma_start(out=wg_w[:].bitcast(I32), in_=wg_words[0].bitcast(I32))
-        load_scale_rows(wg_s, wg_scales)
-        for e in range(E):
-            nc.sync.dma_start(out=w1_raw[e][:], in_=w1[e].rearrange("(p j) c -> p j c", j=PACK))
-        for lo, hi in GROUPS:
-            nc.sync.dma_start(out=w2_raw[:, lo:hi], in_=w2[lo:hi].rearrange("e (p j) c -> p e j c", j=PACK))
-        nc.sync.dma_start(pos_t[0][:], pos1)
-        nc.sync.dma_start(pos_t[1][:], pos2)
-        nc.sync.dma_start(out=gate_t[:], in_=gate.rearrange("r p t -> p r t"))
-
-        for lo, hi in GATHER_CUTS:
+        def gather(words, scales, lo, hi):
             entries = offs_t[:, lo // LIST_ROWS : hi // LIST_ROWS]
-            nc.vector.tensor_copy(slot_w[:, lo:hi], x_w[:].indirect(entries))
-            nc.vector.tensor_copy(slot_s[:, lo:hi], x_s[:].indirect(entries))
+            nc.vector.tensor_copy(words, x_w[:].indirect(entries))
+            nc.vector.tensor_copy(scales, x_s[:].indirect(entries))
 
         def round_w1(e):
-            src = w1_raw[e][:].rearrange("p j (m t) -> p m j t", t=PACK)
-            dst = w1_b[e][:].rearrange("p t m j -> p m j t")
-            lo, hi = W1_ON_VECTOR[e]
-            if lo > 0:
-                nc.scalar.copy(out=dst[:, 0:lo], in_=src[:, 0:lo])
-            if hi > lo:
-                nc.vector.tensor_copy(out=dst[:, lo:hi], in_=src[:, lo:hi])
-            if hi < P:
-                nc.scalar.copy(out=dst[:, hi:P], in_=src[:, hi:P])
+            for u in range(2):
+                src = w1_raw[e][:].rearrange("p j (m t) -> p m j t", t=PACK)[:, :, :, 2 * u : 2 * u + 2]
+                dst = w1_b[e][u][:].rearrange("p t m j -> p m j t")
+                cut = W1_ON_VECTOR[e][u]
+                if cut > 0:
+                    nc.vector.tensor_copy(out=dst[:, 0:cut], in_=src[:, 0:cut])
+                if cut < P:
+                    nc.scalar.copy(out=dst[:, cut:P], in_=src[:, cut:P])
 
-        round_w1(0)
-        for e in range(E):
-            if e + 1 < E:
-                round_w1(e + 1)
-            quantize(w1_w[e][:], w1_s[e][:], w1_b[e][:].rearrange("p t m j -> p (t m j)"))
+        def quantize_w1(e):
+            for u in range(2):
+                cols = slice(2 * P * u, 2 * P * (u + 1))
+                quantize(w1_w[e][:, cols], w1_s[e][:, cols], w1_b[e][u][:].rearrange("p t m j -> p (t m j)"))
 
-        gate_pieces = ((0, BANK), (BANK, T))
-        for turn, (lo, hi) in enumerate(gate_pieces):
-            bank = first_banks[turn][:, 0 : hi - lo]
-            mx_matmul(bank, (wg_w[:].bitcast(FP4X4), wg_s[:]), (x_w[:, lo:hi].bitcast(FP8X4), x_s[:, lo:hi]))
-            nc.scalar.activation(o[:, lo:hi], bank, SILU)
+        def first_layer(e, words, scales, h_b):
+            for half in range(C // BANK_SLOTS):
+                places = slice(half * BANK_SLOTS, (half + 1) * BANK_SLOTS)
+                bank = first_banks[(2 * e + half) % FIRST_BANKS][:].rearrange("p (t s) -> p t s", t=PACK)
+                for t in range(PACK):
+                    cols = slice(t * P, (t + 1) * P)
+                    mx_matmul(
+                        bank[:, t, :],
+                        (w1_w[e][:, cols].bitcast(FP8X4), w1_s[e][:, cols]),
+                        (words[:, places].bitcast(FP8X4), scales[:, places]),
+                    )
+                nc.scalar.activation(h_b[:, places, :], bank.rearrange("p t s -> p s t"), SILU)
 
-        for lo, hi in GROUPS:
-            nc.vector.tensor_copy(
-                out=w2_b[:, lo:hi].rearrange("p e (c d) j -> p e c j d", d=4),
-                in_=w2_raw[:, lo:hi].rearrange("p e j (c d) -> p e c j d", d=4),
+        def quantize_h(h_b, first, tag):
+            slots = h_b.shape[1]
+            h_w = sbuf("h_w%d" % first, [P, slots], U32, tag=tag)
+            quantize(h_w[:], h_s[:, first * C : first * C + slots], h_b.rearrange("p s t -> p (s t)"))
+            return [h_w[:, lo : lo + C] for lo in range(0, slots, C)]
+
+        def round_w2(g):
+            copy = nc.scalar.copy if g + 1 == len(GROUPS) else nc.vector.tensor_copy
+            copy(
+                out=w2_b[g][:].rearrange("p e (c d) j -> p e c j d", d=4),
+                in_=w2_raw[g][:].rearrange("p e j (c d) -> p e c j d", d=4),
             )
 
-        for piece in range(S // BANK_SLOTS):
-            slots = slice(piece * BANK_SLOTS, (piece + 1) * BANK_SLOTS)
-            e = slots.start // C
-            bank = first_banks[(len(gate_pieces) + piece) % FIRST_BANKS][:].rearrange("p (t s) -> p t s", t=PACK)
-            for t in range(PACK):
-                cols = slice(t * P, (t + 1) * P)
-                mx_matmul(
-                    bank[:, t, :],
-                    (w1_w[e][:, cols].bitcast(FP8X4), w1_s[e][:, cols]),
-                    (slot_w[:, slots].bitcast(FP8X4), slot_s[:, slots]),
-                )
-            nc.scalar.activation(h_b[:, slots, :], bank.rearrange("p t s -> p s t"), SILU)
-
-        for turn, (lo, hi) in enumerate(GROUPS):
-            group_cols, group_slots = slice(lo * N, hi * N), slice(lo * C, hi * C)
-            quantize(w2_w[:, group_cols], w2_s[:, group_cols], w2_b[:, lo:hi].rearrange("p e n j -> p (e n j)"))
-            quantize(h_w[:, group_slots], h_s[:, group_slots], h_b[:, group_slots, :].rearrange("p s t -> p (s t)"))
-            bank = second_banks[turn % SECOND_BANKS]
+        def second_layer(g, h_w):
+            lo, hi = GROUPS[g]
+            group_cols = slice(lo * N, hi * N)
+            quantize(w2_w[:, group_cols], w2_s[:, group_cols], w2_b[g][:].rearrange("p e n j -> p (e n j)"))
+            bank = second_banks[g % SECOND_BANKS]
             for e in range(lo, hi):
-                cols, slots = slice(e * N, (e + 1) * N), slice(e * C, (e + 1) * C)
+                cols = slice(e * N, (e + 1) * N)
                 mx_matmul(
                     bank[:, (e - lo) * C : (e - lo + 1) * C],
                     (w2_w[:, cols].bitcast(FP8X4), w2_s[:, cols]),
-                    (h_w[:, slots].bitcast(FP8X4), h_s[:, slots]),
+                    (h_w[e].bitcast(FP8X4), h_s[:, e * C : (e + 1) * C]),
                 )
-            nc.scalar.copy(out=y[:, group_slots], in_=bank[:, 0 : (hi - lo) * C])
+            copy = nc.vector.tensor_copy if g + 1 == len(GROUPS) else nc.scalar.copy
+            copy(out=y[:, lo * C : hi * C], in_=bank[:, 0 : (hi - lo) * C])
 
-        for r in range(2):
-            nc.vector.tensor_tensor(gated[:, r, :], o[:], gate_t[:, r, :], MULT)
+        def slots_of(e):
+            return slot_w[:, e * C : (e + 1) * C], slot_s[:, e * C : (e + 1) * C]
+
+        nc.vector.memset(x_w[:, T:WINDOW].bitcast(I32), 0)
+        nc.vector.memset(x_s[:, T:WINDOW].bitcast(I32), 0)
+        gather(slot_w[:], slot_s[:], 0, S - C)
+        round_w1(0)
+        round_w1(1)
+        quantize_w1(0)
+        last_w = sbuf("last_w", [P, C], U32, tag="w1_b0_0")
+        last_s = sbuf("last_s", [P, C], U8, tag="w1_b0_1")
+        gather(last_w[:], last_s[:], S - C, S)
+        h_01 = sbuf("h_01", [P, 2 * C, PACK], BF16)
+        first_layer(0, *slots_of(0), h_01[:, 0:C, :])
+        round_w1(2)
+        quantize_w1(1)
+        first_layer(1, *slots_of(1), h_01[:, C : 2 * C, :])
+        round_w1(3)
+        quantize_w1(2)
+        h_2 = sbuf("h_2", [P, C, PACK], BF16, tag="w1_raw3")
+        first_layer(2, *slots_of(2), h_2[:])
+        round_w1(4)
+        quantize_w1(3)
+        h_3 = sbuf("h_3", [P, C, PACK], BF16, tag="w1_raw4")
+        first_layer(3, *slots_of(3), h_3[:])
+        quantize_w1(4)
+        h_4 = sbuf("h_4", [P, C, PACK], BF16)
+        first_layer(4, last_w[:], last_s[:], h_4[:])
+        h_w = quantize_h(h_01[:], 0, "w1_b3_0")
+        round_w2(2)
+        round_w2(0)
+        h_w += quantize_h(h_2[:], 2, "w1_b4_0")
+        second_layer(0, h_w)
+        round_w2(1)
+        h_w += quantize_h(h_3[:], 3, None)
+        second_layer(1, h_w)
+        h_w += quantize_h(h_4[:], 4, None)
+        second_layer(2, h_w)
+
+        for bank, (lo, hi) in zip(gate_banks, ((0, BANK), (BANK, T))):
+            z = bank[:, 0 : hi - lo]
+            mx_matmul(z, (wg_w[:].bitcast(FP4X4), wg_s[:]), (x_w[:, lo:hi].bitcast(FP8X4), x_s[:, lo:hi]))
+            nc.scalar.activation(o[:, lo:hi], z, SILU)
 
         def pick(r, lo, hi):
             entries = pos_t[r][:, lo // LIST_ROWS : hi // LIST_ROWS]
-            nc.vector.tensor_tensor(picked[:, r, lo:hi], y[:].indirect(entries), gated[:, r, lo:hi], MULT)
+            nc.vector.tensor_tensor(picked[:, r, lo:hi], y[:].indirect(entries), gate_t[:, r, lo:hi], MULT)
 
-        def add_and_store(lo, hi):
-            nc.vector.tensor_tensor(res[:, lo:hi], picked[:, 0, lo:hi], picked[:, 1, lo:hi], ADD)
+        def add(lo, hi):
+            nc.vector.tensor_tensor(both[:, lo:hi], picked[:, 0, lo:hi], picked[:, 1, lo:hi], ADD)
+
+        def gate_and_store(lo, hi):
+            nc.vector.tensor_tensor(res[:, lo:hi], both[:, lo:hi], o[:, lo:hi], MULT)
             nc.sync.dma_start(out=out[:, lo:hi], in_=res[:, lo:hi])
 
-        for i, (lo, hi) in enumerate(TOKEN_CUTS):
-            pick(0, lo, hi)
-            if i > 0:
-                add_and_store(*TOKEN_CUTS[i - 1])
-            pick(1, lo, hi)
-        add_and_store(*TOKEN_CUTS[-1])
+        pick(0, 0, T)
+        for step in (functools.partial(pick, 1), add, gate_and_store):
+            for lo, hi in TOKEN_CUTS:
+                step(lo, hi)

@@ -27,8 +27,9 @@ BANK_SLOTS = BANK // PACK
 FIRST_BANKS = 4
 SECOND_BANKS = 2
 
-W1_ON_VECTOR = ((0, 0), (0, 64), (P, 64), (P, 40), (P, 40))
-WINDOW = 1408
+W1_ON_VECTOR = ((0, 0), (0, P), (P, 72), (P, 72), (P, 72))
+WORD_WINDOW = 1408
+BYTE_WINDOW = 1792
 GROUPS = ((0, 2), (2, 4), (4, 5))
 TOKEN_CUTS = ((0, T // 2), (T // 2, T))
 
@@ -59,31 +60,32 @@ def tile_moe_ogt_silu_silu_kernel(
             nc.vector.quantize_mx(out=words.bitcast(FP8X4), scales=scales, in_=values)
 
         first_banks = [psum.tile([P, BANK], F32, name="first_bank%d" % b) for b in range(FIRST_BANKS)]
-        second_banks = [psum.tile([P, BANK], F32, name="second_bank%d" % b) for b in range(SECOND_BANKS)]
+        second_banks = [psum.tile([P, BANK], F32, name="second_bank%d" % b) for b in range(2)]
         gate_banks = [psum.tile([P, BANK], F32, name="gate_bank%d" % b) for b in range(2)]
+        second_banks.append(first_banks[2])
 
         offs_t = sbuf("offs_t", [P, S // LIST_ROWS], U16)
         pos_t = [sbuf("pos1_t", [P, T // LIST_ROWS], U16), sbuf("pos2_t", [P, T // LIST_ROWS], U16)]
-        x_w = sbuf("x_w", [P, WINDOW], U32)
-        x_s = sbuf("x_s", [P, WINDOW], U8)
+        x_w = sbuf("x_w", [P, WORD_WINDOW], U32)
+        x_s = sbuf("x_s", [P, BYTE_WINDOW], U8)
         wg_w = sbuf("wg_w", [P, 2 * N], U8)
         wg_s = sbuf("wg_s", [P, N], U8)
         w1_raw = [sbuf("w1_raw%d" % e, [P, PACK, H], F32) for e in range(E)]
         w2_raw = [sbuf("w2_raw%d" % lo, [P, hi - lo, PACK, N], F32) for lo, hi in GROUPS]
         gate_t = sbuf("gate_t", [P, 2, T], F32)
         slot_w = sbuf("slot_w", [P, S - C], U32)
-        slot_s = sbuf("slot_s", [P, S - C], U8)
+        slot_s = sbuf("slot_s", [P, S], U8)
         w1_b = [[sbuf("w1_b%d_%d" % (e, u), [P, 2, P, PACK], BF16) for u in range(2)] for e in range(E)]
         w1_w = [sbuf("w1_w%d" % e, [P, H], U32) for e in range(E)]
         w1_s = [sbuf("w1_s%d" % e, [P, H], U8) for e in range(E)]
-        w2_b = [sbuf("w2_b%d" % lo, [P, hi - lo, N, PACK], BF16) for lo, hi in GROUPS]
+        w2_b = sbuf("w2_b", [P, E, N, PACK], BF16)
         w2_w = sbuf("w2_w", [P, E * N], U32)
         w2_s = sbuf("w2_s", [P, E * N], U8)
         h_s = sbuf("h_s", [P, S], U8)
         y = sbuf("y", [P, S], F32)
         o = sbuf("o", [P, T], F32)
         picked = sbuf("picked", [P, 2, T], F32)
-        both = sbuf("both", [P, T], F32)
+        gated = sbuf("gated", [P, 2, T], F32)
         res = sbuf("res", [P, T], F32)
 
         def load_scale_rows(queues, dst, rows):
@@ -94,27 +96,30 @@ def tile_moe_ogt_silu_silu_kernel(
                     in_=four.unsqueeze(0).to_broadcast([8, 4, four.shape[1]]),
                 )
 
-        nc.sync.dma_start(out=x_w[:, 0:T].bitcast(I32), in_=x_words[0].rearrange("p t d -> p (t d)").bitcast(I32))
+        def load_w2(g):
+            lo, hi = GROUPS[g]
+            nc.sync.dma_start(out=w2_raw[g][:], in_=w2[lo:hi].rearrange("e (p j) c -> p e j c", j=PACK))
+
         nc.sync.dma_start(offs_t[:], offs)
         load_scale_rows((nc.scalar, nc.scalar, nc.sync, nc.sync), x_s[:, 0:T], x_scales)
+        nc.sync.dma_start(out=x_w[:, 0:T].bitcast(I32), in_=x_words[0].rearrange("p t d -> p (t d)").bitcast(I32))
         for e in range(E):
             nc.sync.dma_start(out=w1_raw[e][:], in_=w1[e].rearrange("(p j) c -> p j c", j=PACK))
-        for g, (lo, hi) in enumerate(GROUPS):
-            nc.sync.dma_start(out=w2_raw[g][:], in_=w2[lo:hi].rearrange("e (p j) c -> p e j c", j=PACK))
+        load_w2(2)
         nc.sync.dma_start(out=wg_w[:].bitcast(I32), in_=wg_words[0].bitcast(I32))
         load_scale_rows((nc.sync,) * 4, wg_s[:], wg_scales)
+        load_w2(0)
+        load_w2(1)
+        nc.sync.dma_start(out=gate_t[:], in_=gate.rearrange("r p t -> p r t"))
         nc.sync.dma_start(pos_t[0][:], pos1)
         nc.sync.dma_start(pos_t[1][:], pos2)
-        nc.sync.dma_start(out=gate_t[:], in_=gate.rearrange("r p t -> p r t"))
 
         warm = sbuf("warm", [P, 2], F32)
         nc.vector.memset(warm[:, 0:1], 0.0)
         nc.scalar.activation(warm[:, 1:2], warm[:, 0:1], SILU)
 
-        def gather(words, scales, lo, hi):
-            entries = offs_t[:, lo // LIST_ROWS : hi // LIST_ROWS]
-            nc.vector.tensor_copy(words, x_w[:].indirect(entries))
-            nc.vector.tensor_copy(scales, x_s[:].indirect(entries))
+        def gather(dst, window, lo, hi):
+            nc.vector.tensor_copy(dst, window.indirect(offs_t[:, lo // LIST_ROWS : hi // LIST_ROWS]))
 
         def round_w1(e):
             for u in range(2):
@@ -150,18 +155,19 @@ def tile_moe_ogt_silu_silu_kernel(
             quantize(h_w[:], h_s[:, first * C : first * C + slots], h_b.rearrange("p s t -> p (s t)"))
             return [h_w[:, lo : lo + C] for lo in range(0, slots, C)]
 
-        def round_w2(g):
-            copy = nc.scalar.copy if g + 1 == len(GROUPS) else nc.vector.tensor_copy
+        def round_w2(e, copy):
             copy(
-                out=w2_b[g][:].rearrange("p e (c d) j -> p e c j d", d=4),
-                in_=w2_raw[g][:].rearrange("p e j (c d) -> p e c j d", d=4),
+                out=w2_b[:, e].rearrange("p (c d) j -> p c j d", d=4),
+                in_=w2_raw[e // 2][:, e % 2].rearrange("p j (c d) -> p c j d", d=4),
             )
+
+        def quantize_w2(e):
+            cols = slice(e * N, (e + 1) * N)
+            quantize(w2_w[:, cols], w2_s[:, cols], w2_b[:, e].rearrange("p n j -> p (n j)"))
 
         def second_layer(g, h_w):
             lo, hi = GROUPS[g]
-            group_cols = slice(lo * N, hi * N)
-            quantize(w2_w[:, group_cols], w2_s[:, group_cols], w2_b[g][:].rearrange("p e n j -> p (e n j)"))
-            bank = second_banks[g % SECOND_BANKS]
+            bank = second_banks[g]
             for e in range(lo, hi):
                 cols = slice(e * N, (e + 1) * N)
                 mx_matmul(
@@ -169,65 +175,70 @@ def tile_moe_ogt_silu_silu_kernel(
                     (w2_w[:, cols].bitcast(FP8X4), w2_s[:, cols]),
                     (h_w[e].bitcast(FP8X4), h_s[:, e * C : (e + 1) * C]),
                 )
-            copy = nc.vector.tensor_copy if g + 1 == len(GROUPS) else nc.scalar.copy
-            copy(out=y[:, lo * C : hi * C], in_=bank[:, 0 : (hi - lo) * C])
+            nc.scalar.copy(out=y[:, lo * C : hi * C], in_=bank[:, 0 : (hi - lo) * C])
 
         def slots_of(e):
             return slot_w[:, e * C : (e + 1) * C], slot_s[:, e * C : (e + 1) * C]
 
-        nc.vector.memset(x_w[:, T:WINDOW].bitcast(I32), 0)
-        nc.vector.memset(x_s[:, T:WINDOW].bitcast(I32), 0)
-        gather(slot_w[:], slot_s[:], 0, S - C)
+        nc.vector.memset(x_s[:, T:BYTE_WINDOW].bitcast(I32), 0)
+        nc.vector.memset(x_w[:, T:WORD_WINDOW].bitcast(I32), 0)
+        gather(slot_s[:], x_s[:], 0, S)
+        gather(slot_w[:], x_w[:], 0, S - C)
         round_w1(0)
         round_w1(1)
         quantize_w1(0)
-        last_w = sbuf("last_w", [P, C], U32, tag="w1_b0_0")
-        last_s = sbuf("last_s", [P, C], U8, tag="w1_b0_1")
-        gather(last_w[:], last_s[:], S - C, S)
-        h_01 = sbuf("h_01", [P, 2 * C, PACK], BF16)
-        first_layer(0, *slots_of(0), h_01[:, 0:C, :])
+        last_w = sbuf("last_w", [P, C], U32, tag="w1_b0_1")
+        gather(last_w[:], x_w[:], S - C, S)
+        h_0 = sbuf("h_0", [P, C, PACK], BF16)
+        first_layer(0, *slots_of(0), h_0[:])
         round_w1(2)
         quantize_w1(1)
-        first_layer(1, *slots_of(1), h_01[:, C : 2 * C, :])
+        h_1 = sbuf("h_1", [P, C, PACK], BF16, tag="w1_raw2")
+        first_layer(1, *slots_of(1), h_1[:])
         round_w1(3)
         quantize_w1(2)
         h_2 = sbuf("h_2", [P, C, PACK], BF16, tag="w1_raw3")
         first_layer(2, *slots_of(2), h_2[:])
         round_w1(4)
+        round_w2(4, nc.scalar.copy)
         quantize_w1(3)
         h_3 = sbuf("h_3", [P, C, PACK], BF16, tag="w1_raw4")
         first_layer(3, *slots_of(3), h_3[:])
         quantize_w1(4)
         h_4 = sbuf("h_4", [P, C, PACK], BF16)
-        first_layer(4, last_w[:], last_s[:], h_4[:])
-        h_w = quantize_h(h_01[:], 0, "w1_b3_0")
-        round_w2(2)
-        round_w2(0)
-        h_w += quantize_h(h_2[:], 2, "w1_b4_0")
-        second_layer(0, h_w)
-        round_w2(1)
-        h_w += quantize_h(h_3[:], 3, None)
-        second_layer(1, h_w)
-        h_w += quantize_h(h_4[:], 4, None)
-        second_layer(2, h_w)
+        first_layer(4, last_w[:], slot_s[:, S - C : S], h_4[:])
+        h_w = quantize_h(h_0[:], 0, "w1_b2_0") + quantize_h(h_1[:], 1, "w1_b3_0")
 
         for bank, (lo, hi) in zip(gate_banks, ((0, BANK), (BANK, T))):
             z = bank[:, 0 : hi - lo]
             mx_matmul(z, (wg_w[:].bitcast(FP4X4), wg_s[:]), (x_w[:, lo:hi].bitcast(FP8X4), x_s[:, lo:hi]))
             nc.scalar.activation(o[:, lo:hi], z, SILU)
 
+        h_w += quantize_h(h_2[:], 2, "w1_b4_0")
+        quantize_w2(4)
+        for g, h_next in enumerate((h_3, h_4)):
+            lo, hi = GROUPS[g]
+            round_w2(lo, nc.vector.tensor_copy)
+            round_w2(lo + 1, nc.vector.tensor_copy)
+            quantize_w2(lo)
+            h_w += quantize_h(h_next[:], 3 + g, "w2_raw%d" % lo)
+            quantize_w2(lo + 1)
+        second_layer(0, h_w)
+        second_layer(2, h_w)
+        second_layer(1, h_w)
+
+        for r in range(2):
+            nc.vector.tensor_tensor(gated[:, r, :], o[:], gate_t[:, r, :], MULT)
+
         def pick(r, lo, hi):
             entries = pos_t[r][:, lo // LIST_ROWS : hi // LIST_ROWS]
-            nc.vector.tensor_tensor(picked[:, r, lo:hi], y[:].indirect(entries), gate_t[:, r, lo:hi], MULT)
+            nc.vector.tensor_tensor(picked[:, r, lo:hi], y[:].indirect(entries), gated[:, r, lo:hi], MULT)
 
-        def add(lo, hi):
-            nc.vector.tensor_tensor(both[:, lo:hi], picked[:, 0, lo:hi], picked[:, 1, lo:hi], ADD)
-
-        def gate_and_store(lo, hi):
-            nc.vector.tensor_tensor(res[:, lo:hi], both[:, lo:hi], o[:, lo:hi], MULT)
+        def add_and_store(lo, hi):
+            nc.vector.tensor_tensor(res[:, lo:hi], picked[:, 0, lo:hi], picked[:, 1, lo:hi], ADD)
             nc.sync.dma_start(out=out[:, lo:hi], in_=res[:, lo:hi])
 
         pick(0, 0, T)
-        for step in (functools.partial(pick, 1), add, gate_and_store):
+        for step in (functools.partial(pick, 1), add_and_store):
             for lo, hi in TOKEN_CUTS:
                 step(lo, hi)

@@ -27,7 +27,7 @@ BANK_SLOTS = BANK // PACK
 FIRST_BANKS = 4
 SECOND_BANKS = 2
 
-W1_ON_VECTOR = ((0, 0), (0, P), (P, 72), (P, 72), (P, 72))
+W1_ON_VECTOR = ((0, 0), (0, P), (P, 72), (P, P), (P, 48))
 WORD_WINDOW = 1408
 BYTE_WINDOW = 1792
 GROUPS = ((0, 2), (2, 4), (4, 5))
@@ -82,7 +82,6 @@ def tile_moe_ogt_silu_silu_kernel(
         w2_w = sbuf("w2_w", [P, E * N], U32)
         w2_s = sbuf("w2_s", [P, E * N], U8)
         h_s = sbuf("h_s", [P, S], U8)
-        y = sbuf("y", [P, S], F32)
         o = sbuf("o", [P, T], F32)
         picked = sbuf("picked", [P, 2, T], F32)
         gated = sbuf("gated", [P, 2, T], F32)
@@ -105,11 +104,11 @@ def tile_moe_ogt_silu_silu_kernel(
         nc.sync.dma_start(out=x_w[:, 0:T].bitcast(I32), in_=x_words[0].rearrange("p t d -> p (t d)").bitcast(I32))
         for e in range(E):
             nc.sync.dma_start(out=w1_raw[e][:], in_=w1[e].rearrange("(p j) c -> p j c", j=PACK))
-        load_w2(2)
-        nc.sync.dma_start(out=wg_w[:].bitcast(I32), in_=wg_words[0].bitcast(I32))
-        load_scale_rows((nc.sync,) * 4, wg_s[:], wg_scales)
-        load_w2(0)
-        load_w2(1)
+            if e == 2:
+                nc.sync.dma_start(out=wg_w[:].bitcast(I32), in_=wg_words[0].bitcast(I32))
+                load_scale_rows((nc.sync,) * 4, wg_s[:], wg_scales)
+        for g in range(len(GROUPS)):
+            load_w2(g)
         nc.sync.dma_start(out=gate_t[:], in_=gate.rearrange("r p t -> p r t"))
         nc.sync.dma_start(pos_t[0][:], pos1)
         nc.sync.dma_start(pos_t[1][:], pos2)
@@ -197,35 +196,39 @@ def tile_moe_ogt_silu_silu_kernel(
         first_layer(1, *slots_of(1), h_1[:])
         round_w1(3)
         quantize_w1(2)
-        h_2 = sbuf("h_2", [P, C, PACK], BF16, tag="w1_raw3")
+        h_2 = sbuf("h_2", [P, C, PACK], BF16)
         first_layer(2, *slots_of(2), h_2[:])
-        round_w1(4)
-        round_w2(4, nc.scalar.copy)
-        quantize_w1(3)
-        h_3 = sbuf("h_3", [P, C, PACK], BF16, tag="w1_raw4")
-        first_layer(3, *slots_of(3), h_3[:])
-        quantize_w1(4)
-        h_4 = sbuf("h_4", [P, C, PACK], BF16)
-        first_layer(4, last_w[:], slot_s[:, S - C : S], h_4[:])
-        h_w = quantize_h(h_0[:], 0, "w1_b2_0") + quantize_h(h_1[:], 1, "w1_b3_0")
 
         for bank, (lo, hi) in zip(gate_banks, ((0, BANK), (BANK, T))):
             z = bank[:, 0 : hi - lo]
             mx_matmul(z, (wg_w[:].bitcast(FP4X4), wg_s[:]), (x_w[:, lo:hi].bitcast(FP8X4), x_s[:, lo:hi]))
             nc.scalar.activation(o[:, lo:hi], z, SILU)
 
-        h_w += quantize_h(h_2[:], 2, "w1_b4_0")
+        round_w1(4)
+        quantize_w1(3)
+        h_3 = sbuf("h_3", [P, C, PACK], BF16, tag="w1_raw4")
+        first_layer(3, *slots_of(3), h_3[:])
+        quantize_w1(4)
+        h_4 = sbuf("h_4", [P, C, PACK], BF16)
+        first_layer(4, last_w[:], slot_s[:, S - C : S], h_4[:])
+        round_w2(4, nc.scalar.copy)
+        h_w = quantize_h(h_0[:], 0, "w1_b2_0") + quantize_h(h_1[:], 1, "w1_b3_0")
+
+        h_w += quantize_h(h_2[:], 2, "w1_b3_1")
+        round_w2(0, nc.vector.tensor_copy)
+        round_w2(1, nc.vector.tensor_copy)
+        quantize_w2(0)
+        h_w += quantize_h(h_3[:], 3, "w2_raw0")
+        quantize_w2(1)
+        round_w2(2, nc.vector.tensor_copy)
+        round_w2(3, nc.vector.tensor_copy)
+        quantize_w2(2)
+        quantize_w2(3)
+        h_w += quantize_h(h_4[:], 4, "w2_raw2")
         quantize_w2(4)
-        for g, h_next in enumerate((h_3, h_4)):
-            lo, hi = GROUPS[g]
-            round_w2(lo, nc.vector.tensor_copy)
-            round_w2(lo + 1, nc.vector.tensor_copy)
-            quantize_w2(lo)
-            h_w += quantize_h(h_next[:], 3 + g, "w2_raw%d" % lo)
-            quantize_w2(lo + 1)
-        second_layer(0, h_w)
-        second_layer(2, h_w)
-        second_layer(1, h_w)
+        y = sbuf("y", [P, S], F32, tag="w2_raw4")
+        for g in range(len(GROUPS)):
+            second_layer(g, h_w)
 
         for r in range(2):
             nc.vector.tensor_tensor(gated[:, r, :], o[:], gate_t[:, r, :], MULT)

@@ -156,8 +156,8 @@ def tile_moe_ogt_silu_silu_kernel(
 
         def round_w2(e, copy):
             copy(
-                out=w2_b[:, e].rearrange("p (c d) j -> p c j d", d=4),
-                in_=w2_raw[e // 2][:, e % 2].rearrange("p j (c d) -> p c j d", d=4),
+                out=w2_b[:, e].rearrange("p (c d) j -> p c j d", d=2),
+                in_=w2_raw[e // 2][:, e % 2].rearrange("p j (c d) -> p c j d", d=2),
             )
 
         def quantize_w2(e):

@@ -146,7 +146,11 @@ def tile_moe_ogt_silu_silu_kernel(
                         (w1_w[e][:, cols].bitcast(FP8X4), w1_s[e][:, cols]),
                         (words[:, places].bitcast(FP8X4), scales[:, places]),
                     )
-                nc.scalar.activation(h_b[:, places, :], bank.rearrange("p t s -> p s t"), SILU)
+                nc.scalar.activation(
+                    h_b[:, places, :].rearrange("p (c d) t -> p c t d", d=2),
+                    bank.rearrange("p t (c d) -> p c t d", d=2),
+                    SILU,
+                )
 
         def quantize_h(h_b, first, tag):
             slots = h_b.shape[1]

@@ -1,4 +1,3 @@
-import functools
 from contextlib import ExitStack
 
 import concourse.mybir as mybir
@@ -25,13 +24,16 @@ LIST_ROWS = 16
 BANK = 512
 BANK_SLOTS = BANK // PACK
 FIRST_BANKS = 4
-SECOND_BANKS = 2
 
-W1_ON_VECTOR = ((0, 0), (0, P), (P, 72), (P, P), (P, 48))
-WORD_WINDOW = 1408
+W1_ON_VECTOR = {2: 16, 3: 40, 4: 52}
+WORD_WINDOW = 1024
+EARLY_SLOTS = 2 * C
+W1_ON_GPSIMD = (36, 92)
 BYTE_WINDOW = 1792
 GROUPS = ((0, 2), (2, 4), (4, 5))
 TOKEN_CUTS = ((0, T // 2), (T // 2, T))
+H_HALF = BANK_SLOTS * PACK // 2
+LAP = 16
 
 
 def tile_moe_ogt_silu_silu_kernel(
@@ -60,9 +62,7 @@ def tile_moe_ogt_silu_silu_kernel(
             nc.vector.quantize_mx(out=words.bitcast(FP8X4), scales=scales, in_=values)
 
         first_banks = [psum.tile([P, BANK], F32, name="first_bank%d" % b) for b in range(FIRST_BANKS)]
-        second_banks = [psum.tile([P, BANK], F32, name="second_bank%d" % b) for b in range(2)]
-        gate_banks = [psum.tile([P, BANK], F32, name="gate_bank%d" % b) for b in range(2)]
-        second_banks.append(first_banks[2])
+        second_banks = [psum.tile([P, BANK], F32, name="second_bank%d" % b) for b in range(len(GROUPS))]
 
         offs_t = sbuf("offs_t", [P, S // LIST_ROWS], U16)
         pos_t = [sbuf("pos1_t", [P, T // LIST_ROWS], U16), sbuf("pos2_t", [P, T // LIST_ROWS], U16)]
@@ -70,45 +70,53 @@ def tile_moe_ogt_silu_silu_kernel(
         x_s = sbuf("x_s", [P, BYTE_WINDOW], U8)
         wg_w = sbuf("wg_w", [P, 2 * N], U8)
         wg_s = sbuf("wg_s", [P, N], U8)
-        w1_raw = [sbuf("w1_raw%d" % e, [P, PACK, H], F32) for e in range(E)]
+        raw_lo = H_HALF - LAP
+        raw_hi = raw_lo + PACK * H
+        stage = [sbuf("stage%d" % e, [P, raw_hi - LAP + H_HALF], F32) for e in range(E + 1)]
+        w1_raw = [stage[e][:, raw_lo:raw_hi] for e in range(E)]
+        h_b = [
+            (stage[e + 1][:, 0:H_HALF].bitcast(BF16), stage[e + 1][:, raw_hi - LAP : raw_hi - LAP + H_HALF].bitcast(BF16))
+            for e in range(E)
+        ]
         w2_raw = [sbuf("w2_raw%d" % lo, [P, hi - lo, PACK, N], F32) for lo, hi in GROUPS]
         gate_t = sbuf("gate_t", [P, 2, T], F32)
-        slot_w = sbuf("slot_w", [P, S - C], U32)
+        early_w = sbuf("early_w", [P, EARLY_SLOTS], U32)
         slot_s = sbuf("slot_s", [P, S], U8)
-        w1_b = [[sbuf("w1_b%d_%d" % (e, u), [P, 2, P, PACK], BF16) for u in range(2)] for e in range(E)]
+        w1_b = {e: [sbuf("w1_b%d_%d" % (e, u), [P, 2, P, PACK], BF16)[:] for u in range(2)] for e in range(E) if e != 1}
         w1_w = [sbuf("w1_w%d" % e, [P, H], U32) for e in range(E)]
         w1_s = [sbuf("w1_s%d" % e, [P, H], U8) for e in range(E)]
-        w2_b = sbuf("w2_b", [P, E, N, PACK], BF16)
+        w2_b = [sbuf("w2_b%d" % e, [P, N, PACK], BF16) for e in range(E)]
         w2_w = sbuf("w2_w", [P, E * N], U32)
         w2_s = sbuf("w2_s", [P, E * N], U8)
         h_s = sbuf("h_s", [P, S], U8)
         o = sbuf("o", [P, T], F32)
+        y = sbuf("y", [P, S], F32)
         picked = sbuf("picked", [P, 2, T], F32)
         gated = sbuf("gated", [P, 2, T], F32)
         res = sbuf("res", [P, T], F32)
 
-        def load_scale_rows(queues, dst, rows):
-            for q, queue in enumerate(queues):
-                four = rows[0, 4 * q : 4 * q + 4, :].bitcast(I32)
-                queue.dma_start(
-                    out=dst[32 * q : 32 * q + 32, :].bitcast(I32),
-                    in_=four.unsqueeze(0).to_broadcast([8, 4, four.shape[1]]),
-                )
+        def load_w1(e):
+            nc.sync.dma_start(out=w1_raw[e], in_=w1[e].rearrange("(p j) c -> p (j c)", j=PACK))
 
-        def load_w2(g):
-            lo, hi = GROUPS[g]
-            nc.sync.dma_start(out=w2_raw[g][:], in_=w2[lo:hi].rearrange("e (p j) c -> p e j c", j=PACK))
-
+        nc.vector.memset(wg_s[:].bitcast(I32), 0)
         nc.sync.dma_start(offs_t[:], offs)
-        load_scale_rows((nc.scalar, nc.scalar, nc.sync, nc.sync), x_s[:, 0:T], x_scales)
+        for q, queue in enumerate((nc.scalar, nc.scalar, nc.sync, nc.sync)):
+            four = x_scales[0, 4 * q : 4 * q + 4, :].bitcast(I32)
+            queue.dma_start(
+                out=x_s[32 * q : 32 * q + 32, 0:T].bitcast(I32),
+                in_=four.unsqueeze(0).to_broadcast([8, 4, four.shape[1]]),
+            )
+        load_w1(0)
         nc.sync.dma_start(out=x_w[:, 0:T].bitcast(I32), in_=x_words[0].rearrange("p t d -> p (t d)").bitcast(I32))
-        for e in range(E):
-            nc.sync.dma_start(out=w1_raw[e][:], in_=w1[e].rearrange("(p j) c -> p j c", j=PACK))
-            if e == 2:
-                nc.sync.dma_start(out=wg_w[:].bitcast(I32), in_=wg_words[0].bitcast(I32))
-                load_scale_rows((nc.sync,) * 4, wg_s[:], wg_scales)
-        for g in range(len(GROUPS)):
-            load_w2(g)
+        nc.sync.dma_start(out=wg_w[:].bitcast(I32), in_=wg_words[0].bitcast(I32))
+        for q in range(4):
+            nc.sync.dma_start(
+                out=wg_s[32 * q : 32 * q + 4, :].bitcast(I32), in_=wg_scales[0, 4 * q : 4 * q + 4, :].bitcast(I32)
+            )
+        for e in range(1, E):
+            load_w1(e)
+        for g, (lo, hi) in enumerate(GROUPS):
+            nc.sync.dma_start(out=w2_raw[g][:], in_=w2[lo:hi].rearrange("e (p j) c -> p e j c", j=PACK))
         nc.sync.dma_start(out=gate_t[:], in_=gate.rearrange("r p t -> p r t"))
         nc.sync.dma_start(pos_t[0][:], pos1)
         nc.sync.dma_start(pos_t[1][:], pos2)
@@ -120,22 +128,21 @@ def tile_moe_ogt_silu_silu_kernel(
         def gather(dst, window, lo, hi):
             nc.vector.tensor_copy(dst, window.indirect(offs_t[:, lo // LIST_ROWS : hi // LIST_ROWS]))
 
-        def round_w1(e):
-            for u in range(2):
-                src = w1_raw[e][:].rearrange("p j (m t) -> p m j t", t=PACK)[:, :, :, 2 * u : 2 * u + 2]
-                dst = w1_b[e][u][:].rearrange("p t m j -> p m j t")
-                cut = W1_ON_VECTOR[e][u]
-                if cut > 0:
-                    nc.vector.tensor_copy(out=dst[:, 0:cut], in_=src[:, 0:cut])
-                if cut < P:
-                    nc.scalar.copy(out=dst[:, cut:P], in_=src[:, cut:P])
+        def round_w1(copy, e, u, lo, hi):
+            src = w1_raw[e].rearrange("p (j m t) -> p m j t", j=PACK, t=PACK)[:, lo:hi, :, 2 * u : 2 * u + 2]
+            copy(out=w1_b[e][u].rearrange("p t m j -> p m j t")[:, lo:hi], in_=src)
+
+        def share_w1(e):
+            round_w1(nc.vector.tensor_copy, e, 0, 0, P)
+            round_w1(nc.vector.tensor_copy, e, 1, 0, W1_ON_VECTOR[e])
+            round_w1(nc.scalar.copy, e, 1, W1_ON_VECTOR[e], P)
 
         def quantize_w1(e):
             for u in range(2):
                 cols = slice(2 * P * u, 2 * P * (u + 1))
-                quantize(w1_w[e][:, cols], w1_s[e][:, cols], w1_b[e][u][:].rearrange("p t m j -> p (t m j)"))
+                quantize(w1_w[e][:, cols], w1_s[e][:, cols], w1_b[e][u].rearrange("p t m j -> p (t m j)"))
 
-        def first_layer(e, words, scales, h_b):
+        def first_layer(e, words, scales):
             for half in range(C // BANK_SLOTS):
                 places = slice(half * BANK_SLOTS, (half + 1) * BANK_SLOTS)
                 bank = first_banks[(2 * e + half) % FIRST_BANKS][:].rearrange("p (t s) -> p t s", t=PACK)
@@ -147,92 +154,91 @@ def tile_moe_ogt_silu_silu_kernel(
                         (words[:, places].bitcast(FP8X4), scales[:, places]),
                     )
                 nc.scalar.activation(
-                    h_b[:, places, :].rearrange("p (c d) t -> p c t d", d=2),
+                    h_b[e][half].rearrange("p (c d t) -> p c t d", d=2, t=PACK),
                     bank.rearrange("p t (c d) -> p c t d", d=2),
                     SILU,
                 )
 
-        def quantize_h(h_b, first, tag):
-            slots = h_b.shape[1]
-            h_w = sbuf("h_w%d" % first, [P, slots], U32, tag=tag)
-            quantize(h_w[:], h_s[:, first * C : first * C + slots], h_b.rearrange("p s t -> p (s t)"))
-            return [h_w[:, lo : lo + C] for lo in range(0, slots, C)]
+        h_w = {}
 
-        def round_w2(e, copy):
+        def quantize_h(e, tag=None):
+            h_w[e] = sbuf("h_w%d" % e, [P, C], U32, tag=tag)
+            for half in range(2):
+                lo = half * BANK_SLOTS
+                quantize(h_w[e][:, lo : lo + BANK_SLOTS], h_s[:, e * C + lo : e * C + lo + BANK_SLOTS], h_b[e][half])
+
+        def round_w2(copy, e):
             copy(
-                out=w2_b[:, e].rearrange("p (c d) j -> p c j d", d=2),
+                out=w2_b[e][:].rearrange("p (c d) j -> p c j d", d=2),
                 in_=w2_raw[e // 2][:, e % 2].rearrange("p j (c d) -> p c j d", d=2),
             )
 
         def quantize_w2(e):
             cols = slice(e * N, (e + 1) * N)
-            quantize(w2_w[:, cols], w2_s[:, cols], w2_b[:, e].rearrange("p n j -> p (n j)"))
+            quantize(w2_w[:, cols], w2_s[:, cols], w2_b[e][:].rearrange("p n j -> p (n j)"))
 
-        def second_layer(g, h_w):
+        def second_layer(g, width):
             lo, hi = GROUPS[g]
             bank = second_banks[g]
-            for e in range(lo, hi):
+            for first in range(lo * C, hi * C, width):
+                e = first // C
                 cols = slice(e * N, (e + 1) * N)
                 mx_matmul(
-                    bank[:, (e - lo) * C : (e - lo + 1) * C],
+                    bank[:, first - lo * C : first - lo * C + width],
                     (w2_w[:, cols].bitcast(FP8X4), w2_s[:, cols]),
-                    (h_w[e].bitcast(FP8X4), h_s[:, e * C : (e + 1) * C]),
+                    (h_w[e][:, first - e * C : first - e * C + width].bitcast(FP8X4), h_s[:, first : first + width]),
                 )
             nc.scalar.copy(out=y[:, lo * C : hi * C], in_=bank[:, 0 : (hi - lo) * C])
 
         def slots_of(e):
-            return slot_w[:, e * C : (e + 1) * C], slot_s[:, e * C : (e + 1) * C]
+            words = early_w[:, e * C : (e + 1) * C] if e < 2 else late_w[:, (e - 2) * C : (e - 1) * C]
+            return words, slot_s[:, e * C : (e + 1) * C]
 
         nc.vector.memset(x_s[:, T:BYTE_WINDOW].bitcast(I32), 0)
         nc.vector.memset(x_w[:, T:WORD_WINDOW].bitcast(I32), 0)
         gather(slot_s[:], x_s[:], 0, S)
-        gather(slot_w[:], x_w[:], 0, S - C)
-        round_w1(0)
-        round_w1(1)
-        quantize_w1(0)
-        last_w = sbuf("last_w", [P, C], U32, tag="w1_b0_1")
-        gather(last_w[:], x_w[:], S - C, S)
-        h_0 = sbuf("h_0", [P, C, PACK], BF16)
-        first_layer(0, *slots_of(0), h_0[:])
-        round_w1(2)
-        quantize_w1(1)
-        h_1 = sbuf("h_1", [P, C, PACK], BF16, tag="w1_raw2")
-        first_layer(1, *slots_of(1), h_1[:])
-        round_w1(3)
-        quantize_w1(2)
-        h_2 = sbuf("h_2", [P, C, PACK], BF16)
-        first_layer(2, *slots_of(2), h_2[:])
-
-        for bank, (lo, hi) in zip(gate_banks, ((0, BANK), (BANK, T))):
+        gather(early_w[:], x_w[:], 0, EARLY_SLOTS)
+        for u in range(2):
+            round_w1(nc.scalar.copy, 0, u, 0, P)
+        for bank, (lo, hi) in zip(first_banks, ((0, BANK), (BANK, T))):
             z = bank[:, 0 : hi - lo]
             mx_matmul(z, (wg_w[:].bitcast(FP4X4), wg_s[:]), (x_w[:, lo:hi].bitcast(FP8X4), x_s[:, lo:hi]))
             nc.scalar.activation(o[:, lo:hi], z, SILU)
-
-        round_w1(4)
-        quantize_w1(3)
-        h_3 = sbuf("h_3", [P, C, PACK], BF16, tag="w1_raw4")
-        first_layer(3, *slots_of(3), h_3[:])
-        quantize_w1(4)
-        h_4 = sbuf("h_4", [P, C, PACK], BF16)
-        first_layer(4, last_w[:], slot_s[:, S - C : S], h_4[:])
-        round_w2(4, nc.scalar.copy)
-        h_w = quantize_h(h_0[:], 0, "w1_b2_0") + quantize_h(h_1[:], 1, "w1_b3_0")
-
-        h_w += quantize_h(h_2[:], 2, "w1_b3_1")
-        round_w2(0, nc.vector.tensor_copy)
-        round_w2(1, nc.vector.tensor_copy)
+        quantize_w1(0)
+        late_w = sbuf("late_w", [P, S - EARLY_SLOTS], U32, tag="stage0")
+        gather(late_w[:], x_w[:], EARLY_SLOTS, S)
+        whole = sbuf("w1_b1", [P, PACK, P, PACK], BF16, tag="w1_b0_1")
+        w1_b[1] = [whole[:, 0:2], whole[:, 2:4]]
+        src = w1_raw[1].rearrange("p (j m t) -> p m j t", j=PACK, t=PACK)
+        dst = whole[:].rearrange("p t m j -> p m j t")
+        lo, hi = W1_ON_GPSIMD
+        order = "p m j t -> p m t j"
+        nc.gpsimd.tensor_scalar(dst[:, lo:hi].rearrange(order), src[:, lo:hi].rearrange(order), 1.0, 0.0, MULT, ADD)
+        nc.scalar.copy(out=dst[:, 0:lo], in_=src[:, 0:lo])
+        nc.scalar.copy(out=dst[:, hi:P], in_=src[:, hi:P])
+        first_layer(0, *slots_of(0))
+        quantize_w1(1)
+        for e in range(2, E):
+            share_w1(e)
+            first_layer(e - 1, *slots_of(e - 1))
+            quantize_w1(e)
+            quantize_h(e - 2, "w1_b%d_0" % e)
+        round_w2(nc.scalar.copy, 0)
+        first_layer(E - 1, *slots_of(E - 1))
+        round_w2(nc.vector.tensor_copy, 1)
+        quantize_h(3)
+        round_w2(nc.vector.tensor_copy, 2)
+        round_w2(nc.vector.tensor_copy, 3)
         quantize_w2(0)
-        h_w += quantize_h(h_3[:], 3, "w2_raw0")
         quantize_w2(1)
-        round_w2(2, nc.vector.tensor_copy)
-        round_w2(3, nc.vector.tensor_copy)
+        round_w2(nc.vector.tensor_copy, 4)
         quantize_w2(2)
         quantize_w2(3)
-        h_w += quantize_h(h_4[:], 4, "w2_raw2")
         quantize_w2(4)
-        y = sbuf("y", [P, S], F32, tag="w2_raw4")
-        for g in range(len(GROUPS)):
-            second_layer(g, h_w)
+        quantize_h(4)
+        second_layer(0, C)
+        second_layer(1, C)
+        second_layer(2, C // 2)
 
         for r in range(2):
             nc.vector.tensor_tensor(gated[:, r, :], o[:], gate_t[:, r, :], MULT)
@@ -241,11 +247,9 @@ def tile_moe_ogt_silu_silu_kernel(
             entries = pos_t[r][:, lo // LIST_ROWS : hi // LIST_ROWS]
             nc.vector.tensor_tensor(picked[:, r, lo:hi], y[:].indirect(entries), gated[:, r, lo:hi], MULT)
 
-        def add_and_store(lo, hi):
+        pick(0, 0, T)
+        for lo, hi in TOKEN_CUTS:
+            pick(1, lo, hi)
+        for lo, hi in TOKEN_CUTS:
             nc.vector.tensor_tensor(res[:, lo:hi], picked[:, 0, lo:hi], picked[:, 1, lo:hi], ADD)
             nc.sync.dma_start(out=out[:, lo:hi], in_=res[:, lo:hi])
-
-        pick(0, 0, T)
-        for step in (functools.partial(pick, 1), add_and_store):
-            for lo, hi in TOKEN_CUTS:
-                step(lo, hi)

@@ -15,6 +15,7 @@ U8 = mybir.dt.uint8
 FP8X4 = mybir.dt.float8_e4m3fn_x4
 FP4X4 = mybir.dt.float4_e2m1fn_x4
 SILU = mybir.ActivationFunctionType.Silu
+COPY = mybir.ActivationFunctionType.Copy
 MULT = mybir.AluOpType.mult
 ADD = mybir.AluOpType.add
 
@@ -247,9 +248,26 @@ def tile_moe_ogt_silu_silu_kernel(
             entries = pos_t[r][:, lo // LIST_ROWS : hi // LIST_ROWS]
             nc.vector.tensor_tensor(picked[:, r, lo:hi], y[:].indirect(entries), gated[:, r, lo:hi], MULT)
 
-        pick(0, 0, T)
-        for lo, hi in TOKEN_CUTS:
-            pick(1, lo, hi)
-        for lo, hi in TOKEN_CUTS:
+        fetched = sbuf("fetched", [P, 2, T], F32)
+
+        def fetch(r, lo, hi):
+            entries = pos_t[r][:, lo // LIST_ROWS : hi // LIST_ROWS]
+            nc.scalar.activation(fetched[:, r, lo:hi], y[:].indirect(entries), COPY)
+
+        def weigh(r, lo, hi):
+            nc.vector.tensor_tensor(picked[:, r, lo:hi], fetched[:, r, lo:hi], gated[:, r, lo:hi], MULT)
+
+        def finish(lo, hi):
             nc.vector.tensor_tensor(res[:, lo:hi], picked[:, 0, lo:hi], picked[:, 1, lo:hi], ADD)
             nc.sync.dma_start(out=out[:, lo:hi], in_=res[:, lo:hi])
+
+        half = T // 2
+        fetch(1, 0, half)
+        fetch(1, half, T)
+        fetch(0, half, T)
+        pick(0, 0, half)
+        weigh(1, 0, half)
+        weigh(1, half, T)
+        finish(0, half)
+        weigh(0, half, T)
+        finish(half, T)

@@ -254,20 +254,22 @@ def tile_moe_ogt_silu_silu_kernel(
             entries = pos_t[r][:, lo // LIST_ROWS : hi // LIST_ROWS]
             nc.scalar.activation(fetched[:, r, lo:hi], y[:].indirect(entries), COPY)
 
-        def weigh(r, lo, hi):
-            nc.vector.tensor_tensor(picked[:, r, lo:hi], fetched[:, r, lo:hi], gated[:, r, lo:hi], MULT)
+        def weigh(rows, lo, hi):
+            nc.vector.tensor_tensor(picked[:, rows, lo:hi], fetched[:, rows, lo:hi], gated[:, rows, lo:hi], MULT)
 
         def finish(lo, hi):
             nc.vector.tensor_tensor(res[:, lo:hi], picked[:, 0, lo:hi], picked[:, 1, lo:hi], ADD)
             nc.sync.dma_start(out=out[:, lo:hi], in_=res[:, lo:hi])
 
-        half = T // 2
-        fetch(1, 0, half)
-        fetch(1, half, T)
-        fetch(0, half, T)
-        pick(0, 0, half)
-        weigh(1, 0, half)
-        weigh(1, half, T)
-        finish(0, half)
-        weigh(0, half, T)
-        finish(half, T)
+        fetch(1, 0, 256)
+        fetch(1, 256, 512)
+        fetch(0, 512, T)
+        fetch(1, 512, T)
+        pick(0, 0, 256)
+        weigh(1, 0, 256)
+        pick(0, 256, 512)
+        finish(0, 256)
+        weigh(1, 256, 512)
+        weigh(slice(0, 2), 512, T)
+        finish(256, 512)
+        finish(512, T)

@@ -23,18 +23,17 @@ P = 128
 PACK = 4
 LIST_ROWS = 16
 BANK = 512
-BANK_SLOTS = BANK // PACK
-FIRST_BANKS = 4
-
-W1_ON_VECTOR = {2: 16, 3: 40, 4: 52}
-WORD_WINDOW = 1024
-EARLY_SLOTS = 2 * C
-W1_ON_GPSIMD = (36, 92)
+HALF = C // 2
+RING = 4
+EARLY_SLOTS = 256
+WORD_WINDOW = 1408
 BYTE_WINDOW = 1792
+W1_ON_GPSIMD = {0: (44,96), 1: (28,100)}
+W1_ON_VECTOR = {2: 16, 3: 32, 4: 52}
 GROUPS = ((0, 2), (2, 4), (4, 5))
-TOKEN_CUTS = ((0, T // 2), (T // 2, T))
-H_HALF = BANK_SLOTS * PACK // 2
-LAP = 16
+LAP = 2
+RAW = PACK * H
+SECOND_H = C + RAW - 16
 
 
 def tile_moe_ogt_silu_silu_kernel(
@@ -62,8 +61,8 @@ def tile_moe_ogt_silu_silu_kernel(
         def quantize(words, scales, values):
             nc.vector.quantize_mx(out=words.bitcast(FP8X4), scales=scales, in_=values)
 
-        first_banks = [psum.tile([P, BANK], F32, name="first_bank%d" % b) for b in range(FIRST_BANKS)]
-        second_banks = [psum.tile([P, BANK], F32, name="second_bank%d" % b) for b in range(len(GROUPS))]
+        ring = [psum.tile([P, BANK], F32, name="ring%d" % b) for b in range(RING)]
+        second_banks = [psum.tile([P, BANK], F32, name="second_bank%d" % b) for b in range(4)]
 
         offs_t = sbuf("offs_t", [P, S // LIST_ROWS], U16)
         pos_t = [sbuf("pos1_t", [P, T // LIST_ROWS], U16), sbuf("pos2_t", [P, T // LIST_ROWS], U16)]
@@ -71,19 +70,18 @@ def tile_moe_ogt_silu_silu_kernel(
         x_s = sbuf("x_s", [P, BYTE_WINDOW], U8)
         wg_w = sbuf("wg_w", [P, 2 * N], U8)
         wg_s = sbuf("wg_s", [P, N], U8)
-        raw_lo = H_HALF - LAP
-        raw_hi = raw_lo + PACK * H
-        stage = [sbuf("stage%d" % e, [P, raw_hi - LAP + H_HALF], F32) for e in range(E + 1)]
-        w1_raw = [stage[e][:, raw_lo:raw_hi] for e in range(E)]
-        h_b = [
-            (stage[e + 1][:, 0:H_HALF].bitcast(BF16), stage[e + 1][:, raw_hi - LAP : raw_hi - LAP + H_HALF].bitcast(BF16))
-            for e in range(E)
-        ]
+        stage = [sbuf("stage%d" % e, [P, SECOND_H + C], F32) for e in range(E + 1)]
+        w1_raw = [stage[e][:, C - LAP : C - LAP + RAW] for e in range(E)]
+        h_b = [(stage[e + 1][:, 0:C].bitcast(BF16), stage[e + 1][:, SECOND_H : SECOND_H + C].bitcast(BF16)) for e in range(E)]
         w2_raw = [sbuf("w2_raw%d" % lo, [P, hi - lo, PACK, N], F32) for lo, hi in GROUPS]
         gate_t = sbuf("gate_t", [P, 2, T], F32)
         early_w = sbuf("early_w", [P, EARLY_SLOTS], U32)
         slot_s = sbuf("slot_s", [P, S], U8)
-        w1_b = {e: [sbuf("w1_b%d_%d" % (e, u), [P, 2, P, PACK], BF16)[:] for u in range(2)] for e in range(E) if e != 1}
+        w1_whole = [sbuf("w1_whole%d" % e, [P, PACK, P, PACK], BF16) for e in range(2)]
+        w1_b = {e: [sbuf("w1_b%d_%d" % (e, u), [P, 2, P, PACK], BF16)[:] for u in range(2)] for e in range(2, E)}
+        for e in range(2):
+            w1_b[e] = [w1_whole[e][:, 0:2], w1_whole[e][:, 2:4]]
+        w1_b[2][0] = w1_b[1][0]
         w1_w = [sbuf("w1_w%d" % e, [P, H], U32) for e in range(E)]
         w1_s = [sbuf("w1_s%d" % e, [P, H], U8) for e in range(E)]
         w2_b = [sbuf("w2_b%d" % e, [P, N, PACK], BF16) for e in range(E)]
@@ -92,6 +90,7 @@ def tile_moe_ogt_silu_silu_kernel(
         h_s = sbuf("h_s", [P, S], U8)
         o = sbuf("o", [P, T], F32)
         y = sbuf("y", [P, S], F32)
+        fetched = sbuf("fetched", [P, 2, T], F32)
         picked = sbuf("picked", [P, 2, T], F32)
         gated = sbuf("gated", [P, 2, T], F32)
         res = sbuf("res", [P, T], F32)
@@ -129,13 +128,23 @@ def tile_moe_ogt_silu_silu_kernel(
         def gather(dst, window, lo, hi):
             nc.vector.tensor_copy(dst, window.indirect(offs_t[:, lo // LIST_ROWS : hi // LIST_ROWS]))
 
+        def round_early(e, low):
+            src = w1_raw[e].rearrange("p (j m t) -> p m j t", j=PACK, t=PACK)
+            dst = w1_whole[e][:].rearrange("p t m j -> p m j t")
+            lo, hi = W1_ON_GPSIMD[e]
+            order = "p m j t -> p m t j"
+            nc.gpsimd.tensor_scalar(dst[:, lo:hi].rearrange(order), src[:, lo:hi].rearrange(order), 1.0, 0.0, MULT, ADD)
+            nc.scalar.copy(out=dst[:, hi:P], in_=src[:, hi:P])
+            low(out=dst[:, 0:lo], in_=src[:, 0:lo])
+
         def round_w1(copy, e, u, lo, hi):
             src = w1_raw[e].rearrange("p (j m t) -> p m j t", j=PACK, t=PACK)[:, lo:hi, :, 2 * u : 2 * u + 2]
             copy(out=w1_b[e][u].rearrange("p t m j -> p m j t")[:, lo:hi], in_=src)
 
-        def share_w1(e):
+        def round_late(e):
             round_w1(nc.vector.tensor_copy, e, 0, 0, P)
-            round_w1(nc.vector.tensor_copy, e, 1, 0, W1_ON_VECTOR[e])
+            if W1_ON_VECTOR[e]:
+                round_w1(nc.vector.tensor_copy, e, 1, 0, W1_ON_VECTOR[e])
             round_w1(nc.scalar.copy, e, 1, W1_ON_VECTOR[e], P)
 
         def quantize_w1(e):
@@ -143,16 +152,17 @@ def tile_moe_ogt_silu_silu_kernel(
                 cols = slice(2 * P * u, 2 * P * (u + 1))
                 quantize(w1_w[e][:, cols], w1_s[e][:, cols], w1_b[e][u].rearrange("p t m j -> p (t m j)"))
 
-        def first_layer(e, words, scales):
-            for half in range(C // BANK_SLOTS):
-                places = slice(half * BANK_SLOTS, (half + 1) * BANK_SLOTS)
-                bank = first_banks[(2 * e + half) % FIRST_BANKS][:].rearrange("p (t s) -> p t s", t=PACK)
+        def first_layer(e):
+            for half in range(2):
+                lo = e * C + half * HALF
+                words = early_w[:, lo : lo + HALF] if lo < EARLY_SLOTS else late_w[:, lo - EARLY_SLOTS : lo - EARLY_SLOTS + HALF]
+                bank = ring[(2 * e + half) % RING][:].rearrange("p (t s) -> p t s", t=PACK)
                 for t in range(PACK):
                     cols = slice(t * P, (t + 1) * P)
                     mx_matmul(
                         bank[:, t, :],
                         (w1_w[e][:, cols].bitcast(FP8X4), w1_s[e][:, cols]),
-                        (words[:, places].bitcast(FP8X4), scales[:, places]),
+                        (words.bitcast(FP8X4), slot_s[:, lo : lo + HALF]),
                     )
                 nc.scalar.activation(
                     h_b[e][half].rearrange("p (c d t) -> p c t d", d=2, t=PACK),
@@ -165,8 +175,8 @@ def tile_moe_ogt_silu_silu_kernel(
         def quantize_h(e, tag=None):
             h_w[e] = sbuf("h_w%d" % e, [P, C], U32, tag=tag)
             for half in range(2):
-                lo = half * BANK_SLOTS
-                quantize(h_w[e][:, lo : lo + BANK_SLOTS], h_s[:, e * C + lo : e * C + lo + BANK_SLOTS], h_b[e][half])
+                lo = half * HALF
+                quantize(h_w[e][:, lo : lo + HALF], h_s[:, e * C + lo : e * C + lo + HALF], h_b[e][half])
 
         def round_w2(copy, e):
             copy(
@@ -178,7 +188,7 @@ def tile_moe_ogt_silu_silu_kernel(
             cols = slice(e * N, (e + 1) * N)
             quantize(w2_w[:, cols], w2_s[:, cols], w2_b[e][:].rearrange("p n j -> p (n j)"))
 
-        def second_layer(g, width):
+        def second_layer(g, width, copy=nc.scalar.copy):
             lo, hi = GROUPS[g]
             bank = second_banks[g]
             for first in range(lo * C, hi * C, width):
@@ -189,43 +199,30 @@ def tile_moe_ogt_silu_silu_kernel(
                     (w2_w[:, cols].bitcast(FP8X4), w2_s[:, cols]),
                     (h_w[e][:, first - e * C : first - e * C + width].bitcast(FP8X4), h_s[:, first : first + width]),
                 )
-            nc.scalar.copy(out=y[:, lo * C : hi * C], in_=bank[:, 0 : (hi - lo) * C])
-
-        def slots_of(e):
-            words = early_w[:, e * C : (e + 1) * C] if e < 2 else late_w[:, (e - 2) * C : (e - 1) * C]
-            return words, slot_s[:, e * C : (e + 1) * C]
+            copy(out=y[:, lo * C : hi * C], in_=bank[:, 0 : (hi - lo) * C])
 
         nc.vector.memset(x_s[:, T:BYTE_WINDOW].bitcast(I32), 0)
         nc.vector.memset(x_w[:, T:WORD_WINDOW].bitcast(I32), 0)
         gather(slot_s[:], x_s[:], 0, S)
         gather(early_w[:], x_w[:], 0, EARLY_SLOTS)
-        for u in range(2):
-            round_w1(nc.scalar.copy, 0, u, 0, P)
-        for bank, (lo, hi) in zip(first_banks, ((0, BANK), (BANK, T))):
+        round_early(0, nc.scalar.copy)
+        for bank, (lo, hi) in zip(ring, ((0, 128), (128, 384), (384, T))):
             z = bank[:, 0 : hi - lo]
             mx_matmul(z, (wg_w[:].bitcast(FP4X4), wg_s[:]), (x_w[:, lo:hi].bitcast(FP8X4), x_s[:, lo:hi]))
             nc.scalar.activation(o[:, lo:hi], z, SILU)
         quantize_w1(0)
         late_w = sbuf("late_w", [P, S - EARLY_SLOTS], U32, tag="stage0")
         gather(late_w[:], x_w[:], EARLY_SLOTS, S)
-        whole = sbuf("w1_b1", [P, PACK, P, PACK], BF16, tag="w1_b0_1")
-        w1_b[1] = [whole[:, 0:2], whole[:, 2:4]]
-        src = w1_raw[1].rearrange("p (j m t) -> p m j t", j=PACK, t=PACK)
-        dst = whole[:].rearrange("p t m j -> p m j t")
-        lo, hi = W1_ON_GPSIMD
-        order = "p m j t -> p m t j"
-        nc.gpsimd.tensor_scalar(dst[:, lo:hi].rearrange(order), src[:, lo:hi].rearrange(order), 1.0, 0.0, MULT, ADD)
-        nc.scalar.copy(out=dst[:, 0:lo], in_=src[:, 0:lo])
-        nc.scalar.copy(out=dst[:, hi:P], in_=src[:, hi:P])
-        first_layer(0, *slots_of(0))
+        round_early(1, nc.scalar.copy)
+        first_layer(0)
         quantize_w1(1)
         for e in range(2, E):
-            share_w1(e)
-            first_layer(e - 1, *slots_of(e - 1))
+            round_late(e)
+            first_layer(e - 1)
             quantize_w1(e)
-            quantize_h(e - 2, "w1_b%d_0" % e)
+            quantize_h(e - 2, "w1_b%d_0" % e if e in (2,3,4,) else None)
         round_w2(nc.scalar.copy, 0)
-        first_layer(E - 1, *slots_of(E - 1))
+        first_layer(E - 1)
         round_w2(nc.vector.tensor_copy, 1)
         quantize_h(3)
         round_w2(nc.vector.tensor_copy, 2)
@@ -239,20 +236,19 @@ def tile_moe_ogt_silu_silu_kernel(
         quantize_h(4)
         second_layer(0, C)
         second_layer(1, C)
-        second_layer(2, C // 2)
+        second_layer(2, HALF)
 
         for r in range(2):
             nc.vector.tensor_tensor(gated[:, r, :], o[:], gate_t[:, r, :], MULT)
 
-        def pick(r, lo, hi):
-            entries = pos_t[r][:, lo // LIST_ROWS : hi // LIST_ROWS]
-            nc.vector.tensor_tensor(picked[:, r, lo:hi], y[:].indirect(entries), gated[:, r, lo:hi], MULT)
+        def entries(r, lo, hi):
+            return pos_t[r][:, lo // LIST_ROWS : hi // LIST_ROWS]
 
-        fetched = sbuf("fetched", [P, 2, T], F32)
+        def pick(r, lo, hi):
+            nc.vector.tensor_tensor(picked[:, r, lo:hi], y[:].indirect(entries(r, lo, hi)), gated[:, r, lo:hi], MULT)
 
         def fetch(r, lo, hi):
-            entries = pos_t[r][:, lo // LIST_ROWS : hi // LIST_ROWS]
-            nc.scalar.activation(fetched[:, r, lo:hi], y[:].indirect(entries), COPY)
+            nc.scalar.activation(fetched[:, r, lo:hi], y[:].indirect(entries(r, lo, hi)), COPY)
 
         def weigh(rows, lo, hi):
             nc.vector.tensor_tensor(picked[:, rows, lo:hi], fetched[:, rows, lo:hi], gated[:, rows, lo:hi], MULT)
@@ -261,15 +257,10 @@ def tile_moe_ogt_silu_silu_kernel(
             nc.vector.tensor_tensor(res[:, lo:hi], picked[:, 0, lo:hi], picked[:, 1, lo:hi], ADD)
             nc.sync.dma_start(out=out[:, lo:hi], in_=res[:, lo:hi])
 
-        fetch(1, 0, 256)
-        fetch(1, 256, 512)
-        fetch(0, 512, T)
-        fetch(1, 512, T)
-        pick(0, 0, 256)
-        weigh(1, 0, 256)
-        pick(0, 256, 512)
-        finish(0, 256)
-        weigh(1, 256, 512)
-        weigh(slice(0, 2), 512, T)
-        finish(256, 512)
-        finish(512, T)
+        fetch(1, 0, 320)
+        fetch(1, 320, T)
+        pick(0, 0, T)
+        weigh(1, 0, 320)
+        weigh(1, 320, T)
+        finish(0, 320)
+        finish(320, T)

@@ -25,8 +25,8 @@ LIST_ROWS = 16
 BANK = 512
 HALF = C // 2
 RING = 4
-EARLY_SLOTS = 256
-WORD_WINDOW = 1408
+EARLY_SLOTS = 512
+WORD_WINDOW = 1024
 BYTE_WINDOW = 1792
 W1_ON_GPSIMD = {0: (44,96), 1: (28,100)}
 W1_ON_VECTOR = {2: 16, 3: 32, 4: 52}

from contextlib import ExitStack

import concourse.mybir as mybir

K, T, E, C, H, N = 512, 640, 5, 256, 512, 128
S = E * C
FLOPS = 2 * K * N * T + 2 * S * (K * H + H * N)

F32 = mybir.dt.float32
BF16 = mybir.dt.bfloat16
I32 = mybir.dt.int32
U32 = mybir.dt.uint32
U16 = mybir.dt.uint16
U8 = mybir.dt.uint8
FP8X4 = mybir.dt.float8_e4m3fn_x4
FP4X4 = mybir.dt.float4_e2m1fn_x4
SILU = mybir.ActivationFunctionType.Silu
COPY = mybir.ActivationFunctionType.Copy
MULT = mybir.AluOpType.mult
ADD = mybir.AluOpType.add

P = 128
PACK = 4
LIST_ROWS = 16
BANK = 512
HALF = C // 2
RING = 4
EARLY_SLOTS = 512
WORD_WINDOW = 1024
BYTE_WINDOW = 1792
W1_ON_GPSIMD = {0: (44,96), 1: (28,100)}
W1_ON_VECTOR = {2: 16, 3: 32, 4: 52}
GROUPS = ((0, 2), (2, 4), (4, 5))
LAP = 2
RAW = PACK * H
SECOND_H = C + RAW - 16


def tile_moe_ogt_silu_silu_kernel(
    tc, x_words, x_scales, wg_words, wg_scales, w1, w2, gate, offs, pos1, pos2, out
):
    nc = tc.nc
    with ExitStack() as ctx:
        keep = ctx.enter_context(tc.tile_pool(name="keep", bufs=1))
        psum = ctx.enter_context(tc.psum_pool(name="psum", bufs=1))

        def sbuf(name, shape, dtype, tag=None):
            return keep.tile(shape, dtype, name=name, tag=tag or name, align_bytes=64)

        def mx_matmul(dst, stationary, moving):
            nc.tensor.matmul_mx(
                out=dst,
                lhsT=stationary[0],
                lhsT_scale=stationary[1],
                rhs=moving[0],
                rhs_scale=moving[1],
                start=True,
                stop=True,
            )

        def quantize(words, scales, values):
            nc.vector.quantize_mx(out=words.bitcast(FP8X4), scales=scales, in_=values)

        ring = [psum.tile([P, BANK], F32, name="ring%d" % b) for b in range(RING)]
        second_banks = [psum.tile([P, BANK], F32, name="second_bank%d" % b) for b in range(4)]

        offs_t = sbuf("offs_t", [P, S // LIST_ROWS], U16)
        pos_t = [sbuf("pos1_t", [P, T // LIST_ROWS], U16), sbuf("pos2_t", [P, T // LIST_ROWS], U16)]
        x_w = sbuf("x_w", [P, WORD_WINDOW], U32)
        x_s = sbuf("x_s", [P, BYTE_WINDOW], U8)
        wg_w = sbuf("wg_w", [P, 2 * N], U8)
        wg_s = sbuf("wg_s", [P, N], U8)
        stage = [sbuf("stage%d" % e, [P, SECOND_H + C], F32) for e in range(E + 1)]
        w1_raw = [stage[e][:, C - LAP : C - LAP + RAW] for e in range(E)]
        h_b = [(stage[e + 1][:, 0:C].bitcast(BF16), stage[e + 1][:, SECOND_H : SECOND_H + C].bitcast(BF16)) for e in range(E)]
        w2_raw = [sbuf("w2_raw%d" % lo, [P, hi - lo, PACK, N], F32) for lo, hi in GROUPS]
        gate_t = sbuf("gate_t", [P, 2, T], F32)
        early_w = sbuf("early_w", [P, EARLY_SLOTS], U32)
        slot_s = sbuf("slot_s", [P, S], U8)
        w1_whole = [sbuf("w1_whole%d" % e, [P, PACK, P, PACK], BF16) for e in range(2)]
        w1_b = {e: [sbuf("w1_b%d_%d" % (e, u), [P, 2, P, PACK], BF16)[:] for u in range(2)] for e in range(2, E)}
        for e in range(2):
            w1_b[e] = [w1_whole[e][:, 0:2], w1_whole[e][:, 2:4]]
        w1_b[2][0] = w1_b[1][0]
        w1_w = [sbuf("w1_w%d" % e, [P, H], U32) for e in range(E)]
        w1_s = [sbuf("w1_s%d" % e, [P, H], U8) for e in range(E)]
        w2_b = [sbuf("w2_b%d" % e, [P, N, PACK], BF16) for e in range(E)]
        w2_w = sbuf("w2_w", [P, E * N], U32)
        w2_s = sbuf("w2_s", [P, E * N], U8)
        h_s = sbuf("h_s", [P, S], U8)
        o = sbuf("o", [P, T], F32)
        y = sbuf("y", [P, S], F32)
        fetched = sbuf("fetched", [P, 2, T], F32)
        picked = sbuf("picked", [P, 2, T], F32)
        gated = sbuf("gated", [P, 2, T], F32)
        res = sbuf("res", [P, T], F32)

        def load_w1(e):
            nc.sync.dma_start(out=w1_raw[e], in_=w1[e].rearrange("(p j) c -> p (j c)", j=PACK))

        nc.vector.memset(wg_s[:].bitcast(I32), 0)
        nc.sync.dma_start(offs_t[:], offs)
        for q, queue in enumerate((nc.scalar, nc.scalar, nc.sync, nc.sync)):
            four = x_scales[0, 4 * q : 4 * q + 4, :].bitcast(I32)
            queue.dma_start(
                out=x_s[32 * q : 32 * q + 32, 0:T].bitcast(I32),
                in_=four.unsqueeze(0).to_broadcast([8, 4, four.shape[1]]),
            )
        load_w1(0)
        nc.sync.dma_start(out=x_w[:, 0:T].bitcast(I32), in_=x_words[0].rearrange("p t d -> p (t d)").bitcast(I32))
        nc.sync.dma_start(out=wg_w[:].bitcast(I32), in_=wg_words[0].bitcast(I32))
        for q in range(4):
            nc.sync.dma_start(
                out=wg_s[32 * q : 32 * q + 4, :].bitcast(I32), in_=wg_scales[0, 4 * q : 4 * q + 4, :].bitcast(I32)
            )
        for e in range(1, E):
            load_w1(e)
        for g, (lo, hi) in enumerate(GROUPS):
            nc.sync.dma_start(out=w2_raw[g][:], in_=w2[lo:hi].rearrange("e (p j) c -> p e j c", j=PACK))
        nc.sync.dma_start(out=gate_t[:], in_=gate.rearrange("r p t -> p r t"))
        nc.sync.dma_start(pos_t[0][:], pos1)
        nc.sync.dma_start(pos_t[1][:], pos2)

        warm = sbuf("warm", [P, 2], F32)
        nc.vector.memset(warm[:, 0:1], 0.0)
        nc.scalar.activation(warm[:, 1:2], warm[:, 0:1], SILU)

        def gather(dst, window, lo, hi):
            nc.vector.tensor_copy(dst, window.indirect(offs_t[:, lo // LIST_ROWS : hi // LIST_ROWS]))

        def round_early(e, low):
            src = w1_raw[e].rearrange("p (j m t) -> p m j t", j=PACK, t=PACK)
            dst = w1_whole[e][:].rearrange("p t m j -> p m j t")
            lo, hi = W1_ON_GPSIMD[e]
            order = "p m j t -> p m t j"
            nc.gpsimd.tensor_scalar(dst[:, lo:hi].rearrange(order), src[:, lo:hi].rearrange(order), 1.0, 0.0, MULT, ADD)
            nc.scalar.copy(out=dst[:, hi:P], in_=src[:, hi:P])
            low(out=dst[:, 0:lo], in_=src[:, 0:lo])

        def round_w1(copy, e, u, lo, hi):
            src = w1_raw[e].rearrange("p (j m t) -> p m j t", j=PACK, t=PACK)[:, lo:hi, :, 2 * u : 2 * u + 2]
            copy(out=w1_b[e][u].rearrange("p t m j -> p m j t")[:, lo:hi], in_=src)

        def round_late(e):
            round_w1(nc.vector.tensor_copy, e, 0, 0, P)
            if W1_ON_VECTOR[e]:
                round_w1(nc.vector.tensor_copy, e, 1, 0, W1_ON_VECTOR[e])
            round_w1(nc.scalar.copy, e, 1, W1_ON_VECTOR[e], P)

        def quantize_w1(e):
            for u in range(2):
                cols = slice(2 * P * u, 2 * P * (u + 1))
                quantize(w1_w[e][:, cols], w1_s[e][:, cols], w1_b[e][u].rearrange("p t m j -> p (t m j)"))

        def first_layer(e):
            for half in range(2):
                lo = e * C + half * HALF
                words = early_w[:, lo : lo + HALF] if lo < EARLY_SLOTS else late_w[:, lo - EARLY_SLOTS : lo - EARLY_SLOTS + HALF]
                bank = ring[(2 * e + half) % RING][:].rearrange("p (t s) -> p t s", t=PACK)
                for t in range(PACK):
                    cols = slice(t * P, (t + 1) * P)
                    mx_matmul(
                        bank[:, t, :],
                        (w1_w[e][:, cols].bitcast(FP8X4), w1_s[e][:, cols]),
                        (words.bitcast(FP8X4), slot_s[:, lo : lo + HALF]),
                    )
                nc.scalar.activation(
                    h_b[e][half].rearrange("p (c d t) -> p c t d", d=2, t=PACK),
                    bank.rearrange("p t (c d) -> p c t d", d=2),
                    SILU,
                )

        h_w = {}

        def quantize_h(e, tag=None):
            h_w[e] = sbuf("h_w%d" % e, [P, C], U32, tag=tag)
            for half in range(2):
                lo = half * HALF
                quantize(h_w[e][:, lo : lo + HALF], h_s[:, e * C + lo : e * C + lo + HALF], h_b[e][half])

        def round_w2(copy, e):
            copy(
                out=w2_b[e][:].rearrange("p (c d) j -> p c j d", d=2),
                in_=w2_raw[e // 2][:, e % 2].rearrange("p j (c d) -> p c j d", d=2),
            )

        def quantize_w2(e):
            cols = slice(e * N, (e + 1) * N)
            quantize(w2_w[:, cols], w2_s[:, cols], w2_b[e][:].rearrange("p n j -> p (n j)"))

        def second_layer(g, width, copy=nc.scalar.copy):
            lo, hi = GROUPS[g]
            bank = second_banks[g]
            for first in range(lo * C, hi * C, width):
                e = first // C
                cols = slice(e * N, (e + 1) * N)
                mx_matmul(
                    bank[:, first - lo * C : first - lo * C + width],
                    (w2_w[:, cols].bitcast(FP8X4), w2_s[:, cols]),
                    (h_w[e][:, first - e * C : first - e * C + width].bitcast(FP8X4), h_s[:, first : first + width]),
                )
            copy(out=y[:, lo * C : hi * C], in_=bank[:, 0 : (hi - lo) * C])

        nc.vector.memset(x_s[:, T:BYTE_WINDOW].bitcast(I32), 0)
        nc.vector.memset(x_w[:, T:WORD_WINDOW].bitcast(I32), 0)
        gather(slot_s[:], x_s[:], 0, S)
        gather(early_w[:], x_w[:], 0, EARLY_SLOTS)
        round_early(0, nc.scalar.copy)
        for bank, (lo, hi) in zip(ring, ((0, 128), (128, 384), (384, T))):
            z = bank[:, 0 : hi - lo]
            mx_matmul(z, (wg_w[:].bitcast(FP4X4), wg_s[:]), (x_w[:, lo:hi].bitcast(FP8X4), x_s[:, lo:hi]))
            nc.scalar.activation(o[:, lo:hi], z, SILU)
        quantize_w1(0)
        late_w = sbuf("late_w", [P, S - EARLY_SLOTS], U32, tag="stage0")
        gather(late_w[:], x_w[:], EARLY_SLOTS, S)
        round_early(1, nc.scalar.copy)
        first_layer(0)
        quantize_w1(1)
        for e in range(2, E):
            round_late(e)
            first_layer(e - 1)
            quantize_w1(e)
            quantize_h(e - 2, "w1_b%d_0" % e if e in (2,3,4,) else None)
        round_w2(nc.scalar.copy, 0)
        first_layer(E - 1)
        round_w2(nc.vector.tensor_copy, 1)
        quantize_h(3)
        round_w2(nc.vector.tensor_copy, 2)
        round_w2(nc.vector.tensor_copy, 3)
        quantize_w2(0)
        quantize_w2(1)
        round_w2(nc.vector.tensor_copy, 4)
        quantize_w2(2)
        quantize_w2(3)
        quantize_w2(4)
        quantize_h(4)
        second_layer(0, C)
        second_layer(1, C)
        second_layer(2, HALF)

        for r in range(2):
            nc.vector.tensor_tensor(gated[:, r, :], o[:], gate_t[:, r, :], MULT)

        def entries(r, lo, hi):
            return pos_t[r][:, lo // LIST_ROWS : hi // LIST_ROWS]

        def pick(r, lo, hi):
            nc.vector.tensor_tensor(picked[:, r, lo:hi], y[:].indirect(entries(r, lo, hi)), gated[:, r, lo:hi], MULT)

        def fetch(r, lo, hi):
            nc.scalar.activation(fetched[:, r, lo:hi], y[:].indirect(entries(r, lo, hi)), COPY)

        def weigh(rows, lo, hi):
            nc.vector.tensor_tensor(picked[:, rows, lo:hi], fetched[:, rows, lo:hi], gated[:, rows, lo:hi], MULT)

        def finish(lo, hi):
            nc.vector.tensor_tensor(res[:, lo:hi], picked[:, 0, lo:hi], picked[:, 1, lo:hi], ADD)
            nc.sync.dma_start(out=out[:, lo:hi], in_=res[:, lo:hi])

        fetch(1, 0, 320)
        fetch(1, 320, T)
        pick(0, 0, T)
        weigh(1, 0, 320)
        weigh(1, 320, T)
        finish(0, 320)
        finish(320, T)
